import numpy as np
import ml_dtypes


def mxq(x, axis, fmt="e4m3"):
    dtype, down = {"e4m3": (ml_dtypes.float8_e4m3fn, 7), "e5m2": (ml_dtypes.float8_e5m2, 14)}[fmt]
    v = np.moveaxis(np.asarray(x, np.float32).astype(ml_dtypes.bfloat16).astype(np.float64), axis, -1)
    blocks = v.reshape(v.shape[:-1] + (-1, 32))
    amax = np.abs(blocks).max(-1, keepdims=True)
    byte = np.maximum(np.where(amax > 0, np.frexp(amax)[1] - 1 + 127, 0) - down, 1)
    scale = np.exp2(byte - 127.0)
    codes = (blocks / scale).astype(np.float32).astype(dtype).astype(np.float64)
    return np.moveaxis((codes * scale).reshape(v.shape), -1, axis)


WIDE = False


def mx_kscale(k):
    if not WIDE:
        return np.ones(k)
    levels = np.array([24, -24, 12, -12, 0])
    if k % 512:
        return np.exp2(np.random.permutation(np.resize(levels, k // 32))).repeat(32)
    a = np.empty((k // 512, 16))
    for p in range(k // 512):
        a[p, :8] = np.random.permutation(np.resize(levels, 8))
        for g in range(8):
            far = levels[np.abs(levels - a[p, g]) >= 10]
            a[p, g + 8] = far[np.random.randint(len(far))]
    return np.exp2(a.ravel()).repeat(32)


def f64(x):
    return np.asarray(x).astype(np.float64)


def striped(idx):
    return np.tile(idx.reshape(-1, 16).T, (8, 1)).astype(np.uint16)


def unstriped(offs):
    return offs[:16].T.reshape(-1).astype(np.int64)


E2M1 = np.array([0.0, 0.5, 1.0, 1.5, 2.0, 3.0, 4.0, 6.0, -0.0, -0.5, -1.0, -1.5, -2.0, -3.0, -4.0, -6.0])


def pack_weight(w, fmt):
    k, n = w.shape
    w = f64(np.asarray(w, np.float32).astype(ml_dtypes.bfloat16)).reshape(k // 32, 32, n)
    amax = np.abs(w).max(1)
    if fmt == "e4m3":
        byte = np.frexp(amax)[1] - 1 + 127 - 7
    else:
        mant, ex = np.frexp(amax / 6.0)
        byte = np.where(mant > 0.5, ex, ex - 1) + 127
    byte = np.clip(np.where(amax > 0, byte, 1), 1, 254)
    scaled = (w * np.exp2(127.0 - byte)[:, None, :]).reshape(k, n).astype(np.float32)
    by_word = np.ascontiguousarray(scaled.reshape(k // 512, 128, 4, n).transpose(0, 1, 3, 2))
    if fmt == "e4m3":
        words = by_word.astype(ml_dtypes.float8_e4m3fn).view(np.uint8)
    else:
        c = by_word.astype(ml_dtypes.float4_e2m1fn).view(np.uint8) & 0xF
        words = (c[..., 0::2] | (c[..., 1::2] << 4)).reshape(k // 512, 128, 2 * n)
    return np.ascontiguousarray(words), np.ascontiguousarray(byte.astype(np.uint8).reshape(k // 512, 16, n))


def unpack_weight(words, scales, fmt):
    g, _, n = scales.shape
    words = np.ascontiguousarray(words).reshape(g, 128, n, -1)
    if fmt == "e4m3":
        vals = words.view(ml_dtypes.float8_e4m3fn).astype(np.float64)
    else:
        nib = np.empty((g, 128, n, 4), np.uint8)
        nib[..., 0::2] = words & 0xF
        nib[..., 1::2] = words >> 4
        vals = E2M1[nib]
    vals = vals * np.repeat(np.exp2(scales.astype(np.float64) - 127.0), 8, axis=1)[..., None]
    return vals.transpose(0, 1, 3, 2).reshape(g * 512, n)


def planes(y):
    n, m = y.shape
    v = y.astype(np.float32).astype(ml_dtypes.bfloat16).astype(np.float64).reshape(n // 32, 32, m)
    top = np.abs(v).max(1)
    byte = np.clip(np.where(top > 0, np.frexp(top)[1] - 1 + 127 - 7, 1), 1, 254)
    codes = (v * np.exp2(127.0 - byte)[:, None, :]).reshape(n, m).astype(np.float32).astype(ml_dtypes.float8_e4m3fn).view(np.uint8)
    words = codes.reshape(n // 512, 128, 4, m).transpose(0, 1, 3, 2)
    return np.ascontiguousarray(words), np.ascontiguousarray(byte.astype(np.uint8).reshape(n // 512, 16, m))


def silu(f):
    return f / (1.0 + np.exp(-np.maximum(f, -700.0)))


K, R, N, T, J = 1024, 1024, 512, 2048, 1024


def setup_inputs():
    n = np.random.standard_normal
    s = mx_kscale(K)[:, None]
    u = mx_kscale(R)[:, None]
    p_tab = pack_weight(n((K, T)) * s, "e4m3")
    p_wd = pack_weight(n((R, N)) / np.sqrt(R) / u, "e4m3")
    return {
        "tab_words": p_tab[0],
        "tab_scales": p_tab[1],
        "ws": (n((K, R)) / np.sqrt(2 * K) / s).astype(np.float32),
        "wt": (n((K, R)) / np.sqrt(2 * K) / s).astype(np.float32),
        "sm": (np.random.uniform(0.5, 2.0, R) * u[:, 0]).astype(np.float32),
        "wd_words": p_wd[0],
        "wd_scales": p_wd[1],
        "gT": (n((N, T))).astype(np.float32),
        "wgo": np.tile(np.random.uniform(0.5, 2.0, J), (128, 1)).astype(np.float32),
        "offs": striped(np.random.permutation(T)[:J]),
        "offs2": striped(np.random.permutation(T)[:J]),
    }


def reference(tab_words, tab_scales, ws, wt, sm, wd_words, wd_scales, gT, wgo, offs, offs2):
    idx = unstriped(offs)
    idx2 = unstriped(offs2)
    tab_ = unpack_weight(tab_words, tab_scales, "e4m3")[:, idx]
    tabb_ = unpack_weight(tab_words, tab_scales, "e4m3")[:, idx2]
    ws_ = mxq(f64(ws), 0, "e4m3")
    wt_ = mxq(f64(wt), 0, "e4m3")
    a = ws_.T @ tab_ + wt_.T @ tabb_
    h = f64(sm)[:, None] * silu(a)
    h_ = mxq(h, 0, "e4m3")
    wd_ = unpack_weight(wd_words, wd_scales, "e4m3")
    y = wd_.T @ h_
    out = np.zeros((N, T))
    out[:, idx2] = f64(wgo)[0] * (y * f64(gT)[:, idx])
    return (out,) + planes(out)

@@ -1,0 +1,317 @@
+from contextlib import ExitStack
+
+import concourse.mybir as mybir
+
+K, R, N, T, J = 1024, 1024, 512, 2048, 1024
+FLOPS = 2 * (2 * K * R * J + R * N * J)
+
+F32 = mybir.dt.float32
+BF16 = mybir.dt.bfloat16
+I32 = mybir.dt.int32
+U32 = mybir.dt.uint32
+U16 = mybir.dt.uint16
+U8 = mybir.dt.uint8
+FP8X4 = mybir.dt.float8_e4m3fn_x4
+MULT = mybir.AluOpType.mult
+SILU = mybir.ActivationFunctionType.Silu
+COPY = mybir.ActivationFunctionType.Copy
+
+P = 128
+PACK = 4
+PASS = P * PACK
+BANK = 512
+CHUNK = 256
+QUARTER = 512
+SCALAR_CASTS = 6
+HALF = J // 2
+
+
+def tile_list_msg_silu_gateP_kernel(
+    tc, tab_words, tab_scales, ws, wt, sm, wd_words, wd_scales, gT, wgo, offs, offs2, out_0, out_1, out_2
+):
+    nc = tc.nc
+    with ExitStack() as ctx:
+        keep = ctx.enter_context(tc.tile_pool(name="keep", bufs=1))
+        ring = ctx.enter_context(tc.tile_pool(name="ring", bufs=1))
+        psum = ctx.enter_context(tc.psum_pool(name="psum", bufs=4))
+
+        src_list = keep.tile([P, J // 16], U16, name="src_list")
+        dst_list = keep.tile([P, J // 16], U16, name="dst_list")
+        lists = (src_list, dst_list)
+        tab_sc = keep.tile([P, T], U8, name="tab_sc", align_bytes=64)
+        wd_sc_raw = keep.tile([P, N], U8, name="wd_sc_raw", align_bytes=64)
+        nc.gpsimd.memset(tab_sc[:].bitcast(I32), 0)
+        nc.gpsimd.memset(wd_sc_raw[:].bitcast(I32), 0)
+
+        def load_scale_rows(queue, tile, scales):
+            for q in range(4):
+                queue.dma_start(
+                    out=tile[32 * q : 32 * q + 8, :].bitcast(I32), in_=scales[:, 4 * q : 4 * q + 4, :].bitcast(I32)
+                )
+
+        nc.sync.dma_start(src_list[:], offs)
+        nc.sync.dma_start(dst_list[:], offs2)
+
+        tab_w = [keep.tile([P, T], I32, name="tab_w%d" % a, align_bytes=64) for a in range(2)]
+
+        def load_tab(a, parts):
+            words = tab_words[a].rearrange("p t i -> p (t i)").bitcast(I32)
+            for q in range(parts):
+                cols = slice(q * T // parts, (q + 1) * T // parts)
+                nc.sync.dma_start(out=tab_w[a][:, cols], in_=words[:, cols])
+
+        pieces = [(b, side, a) for b in range(2) for a in range(2) for side in range(2)]
+        raw = {}
+
+        def load_piece(n, parts=1):
+            b, side, a = pieces[n]
+            w = (ws, wt)[side]
+            raw[n] = ring.tile([P, PACK, PASS], F32, name="w_raw", tag="big", bufs=6, align_bytes=64)
+            rows = w[a * PASS : (a + 1) * PASS, b * PASS : (b + 1) * PASS].rearrange("(p i) c -> p i c", i=PACK)
+            for q in range(parts):
+                slots = slice(q * PACK // parts, (q + 1) * PACK // parts)
+                nc.sync.dma_start(out=raw[n][:, slots, :], in_=rows[:, slots, :])
+
+        sm_sb = keep.tile([P, 2, PACK], F32, name="sm_sb")
+        nc.sync.dma_start(out=sm_sb[:], in_=sm.rearrange("(b p t) -> p b t", p=P, t=PACK))
+        load_tab(0, 4)
+        load_scale_rows(nc.sync, tab_sc, tab_scales)
+        load_piece(0, 2)
+        load_tab(1, 4)
+        load_piece(1)
+        load_piece(2)
+        load_piece(3)
+        load_piece(4)
+        wd_raw = keep.tile([P, 2, N], I32, name="wd_raw", align_bytes=64)
+        nc.sync.dma_start(out=wd_raw[:], in_=wd_words.rearrange("a p n i -> p a (n i)").bitcast(I32))
+        load_scale_rows(nc.sync, wd_sc_raw, wd_scales)
+
+        pages = [keep.tile([P, T], F32, name="page%d" % t) for t in range(PACK)]
+        for t in range(PACK):
+            nc.vector.memset(pages[t][:], 0.0)
+
+        v_words = {}
+        v_scales = {}
+
+        def gather_words(a, half, tag):
+            v_words[a, half] = ring.tile([P, 2, HALF], U32, name="v_words", tag=tag, bufs=1, align_bytes=64)
+            for side in range(2):
+                entries = lists[side][:, half * HALF // 16 : (half + 1) * HALF // 16]
+                nc.vector.tensor_copy(v_words[a, half][:, side, :], tab_w[a][:].bitcast(U32).indirect(entries))
+
+        def gather_scales(half, tag):
+            v_scales[half] = ring.tile([P, 2, HALF], U8, name="v_scales", tag=tag, bufs=1, align_bytes=64)
+            for side in range(2):
+                entries = lists[side][:, half * HALF // 16 : (half + 1) * HALF // 16]
+                nc.vector.tensor_copy(v_scales[half][:, side, :], tab_sc[:].indirect(entries))
+
+        w_codes = {}
+        w_scales = {}
+        w_bf = {}
+
+        def cast_piece(n, tag="qin", bufs=3):
+            w_bf[n] = ring.tile([P, PACK * PASS], BF16, name="w_bf", tag=tag, bufs=bufs, align_bytes=64)
+            dst = w_bf[n][:].rearrange("p (t m i) -> p m i t", t=PACK, i=PACK)
+            src = raw[n][:].rearrange("p i (m t) -> p m i t", t=PACK)
+            if n < SCALAR_CASTS:
+                nc.scalar.copy(dst, src)
+            else:
+                nc.vector.tensor_copy(dst, src)
+
+        def quant_piece(n):
+            w_codes[n] = keep.tile([P, PASS], U32, name="w_codes%d" % n, align_bytes=64)
+            w_scales[n] = keep.tile([P, PASS], U8, name="w_scales%d" % n, align_bytes=64)
+            nc.vector.quantize_mx(out=w_codes[n][:].bitcast(FP8X4), scales=w_scales[n][:], in_=w_bf[n][:])
+
+        gather_words(0, 0, "words00")
+        gather_words(0, 1, "words01")
+        gather_scales(0, "scales0")
+        gather_words(1, 0, "words10")
+        for n in range(2):
+            cast_piece(n)
+            quant_piece(n)
+        cast_piece(2, "words11", 1)
+        quant_piece(2)
+        gather_words(1, 1, "words11")
+        cast_piece(3, "scales1", 1)
+        quant_piece(3)
+        gather_scales(1, "scales1")
+        cast_piece(4)
+        quant_piece(4)
+
+        wd_w = keep.tile([P, 2, N], I32, name="wd_w", align_bytes=64)
+        wd_sc = keep.tile([P, N], U8, name="wd_sc", align_bytes=64)
+        nc.vector.tensor_copy(
+            wd_w[:].rearrange("p a (t m) -> p a m t", t=PACK), wd_raw[:].rearrange("p a (m t) -> p a m t", t=PACK)
+        )
+        nc.vector.tensor_copy(
+            wd_sc[:].rearrange("p (t m) -> p t m", t=PACK), wd_sc_raw[:].rearrange("p (m t) -> p t m", t=PACK)
+        )
+
+        for n in range(5, 8):
+            load_piece(n)
+        wgo_sb = keep.tile([P, J], F32, name="wgo_sb")
+        nc.sync.dma_start(out=wgo_sb[:], in_=wgo)
+        for n in range(5, 8):
+            cast_piece(n)
+            quant_piece(n)
+
+        g_rows = {}
+        gates = {}
+
+        def gate(t, tag):
+            gates[t] = ring.tile([P, J], F32, name="gate", tag=tag, bufs=1, align_bytes=64)
+            nc.vector.tensor_tensor(gates[t][:], g_rows[t][:].indirect(src_list[:]), wgo_sb[:], MULT)
+
+        for t in range(PACK):
+            g_rows[t] = ring.tile([P, T], F32, name="g_rows", tag="big", bufs=6, align_bytes=64)
+            nc.sync.dma_start(out=g_rows[t][:], in_=gT.rearrange("(p t) c -> p t c", t=PACK)[:, t, :])
+        for t in range(PACK - 1):
+            gate(t, "gate%d" % t)
+
+        h_codes = [keep.tile([P, J], U32, name="h_codes%d" % b, align_bytes=64) for b in range(2)]
+        h_scales = [keep.tile([P, J], U8, name="h_scales%d" % b, align_bytes=64) for b in range(2)]
+
+        h_rows = {}
+
+        def activate(b, j0, width, t0):
+            half = j0 // HALF
+            cols = slice(j0 % HALF, j0 % HALF + width)
+            per_bank = BANK // width
+            if t0 == 0:
+                h_rows[b, j0] = ring.tile([P, PACK, width], BF16, name="h_rows", tag="h_rows", bufs=1)
+            bank = psum.tile([P, per_bank, width], F32, name="a_bank", tag="a")
+            for u in range(per_bank):
+                rows = slice((t0 + u) * P, (t0 + u + 1) * P)
+                for s in range(4):
+                    n = 4 * b + s
+                    side, a = pieces[n][1:]
+                    nc.tensor.matmul_mx(
+                        out=bank[:, u, :],
+                        lhsT=w_codes[n][:, rows].bitcast(FP8X4),
+                        lhsT_scale=w_scales[n][:, rows],
+                        rhs=v_words[a, half][:, side, cols].bitcast(FP8X4),
+                        rhs_scale=v_scales[half][4 * a : P, side, cols],
+                        start=(s == 0),
+                        stop=(s == 3),
+                    )
+            act = ring.tile([P, per_bank, width], F32, name="act", tag="act", bufs=2)
+            nc.scalar.activation(act[:], bank[:], SILU)
+            for u in range(per_bank):
+                t = t0 + u
+                nc.scalar.activation(h_rows[b, j0][:, t, :], act[:, u, :], COPY, scale=sm_sb[:, b, t : t + 1])
+
+        def pack(b, j0, width, tag="qin", bufs=3):
+            cols = slice(j0, j0 + width)
+            h_bf = ring.tile([P, PACK * width], BF16, name="h_bf", tag=tag, bufs=bufs, align_bytes=64)
+            nc.scalar.copy(
+                h_bf[:].rearrange("p (c i t) -> p c t i", i=4, t=PACK),
+                h_rows[b, j0][:].rearrange("p t (c i) -> p c t i", i=4),
+            )
+            nc.vector.quantize_mx(out=h_codes[b][:, cols].bitcast(FP8X4), scales=h_scales[b][:, cols], in_=h_bf[:])
+
+        def hidden(b, j0, width):
+            for t0 in range(0, PACK, BANK // width):
+                activate(b, j0, width, t0)
+            pack(b, j0, width)
+
+        y_sb = [keep.tile([P, 2, J], F32, name="y_sb%d" % u) for u in range(2)]
+        y_banks = {}
+
+        def message(c):
+            cols = slice(c * CHUNK, (c + 1) * CHUNK)
+            for u in range(2):
+                bank = psum.tile([P, 2, CHUNK], F32, name="y_bank", tag="y")
+                y_banks[c, u] = bank
+                for e in range(2):
+                    t = 2 * u + e
+                    rows = slice(t * P, (t + 1) * P)
+                    for b in range(2):
+                        nc.tensor.matmul_mx(
+                            out=bank[:, e, :],
+                            lhsT=wd_w[:, b, rows].bitcast(FP8X4),
+                            lhsT_scale=wd_sc[4 * b : P, rows],
+                            rhs=h_codes[b][:, cols].bitcast(FP8X4),
+                            rhs_scale=h_scales[b][:, cols],
+                            start=(b == 0),
+                            stop=(b == 1),
+                        )
+
+        def scatter(t, j0, width):
+            cols = slice(j0, j0 + width)
+            nc.vector.tensor_tensor(
+                pages[t][:].indirect(dst_list[:, j0 // 16 : (j0 + width) // 16]),
+                y_sb[t // 2][:, t % 2, cols],
+                gates[t][:, cols],
+                MULT,
+            )
+
+        def deliver(c, u):
+            cols = slice(c * CHUNK, (c + 1) * CHUNK)
+            nc.scalar.copy(y_sb[u][:, :, cols], y_banks[c, u][:])
+            for t in (2 * u, 2 * u + 1):
+                if t < PACK - 1:
+                    scatter(t, c * CHUNK, CHUNK)
+
+        hidden(0, 0, 512)
+        hidden(1, 0, CHUNK)
+        activate(1, CHUNK, CHUNK, 0)
+        activate(1, CHUNK, CHUNK, 2)
+        message(0)
+        deliver(0, 0)
+        pack(1, CHUNK, CHUNK)
+        deliver(0, 1)
+        message(1)
+        activate(0, 512, 512, 0)
+        activate(0, 512, 512, 1)
+        activate(0, 512, 512, 2)
+        deliver(1, 0)
+        activate(0, 512, 512, 3)
+        pack(0, 512, 512, "gate3", 1)
+        gate(3, "gate3")
+        hidden(1, 2 * CHUNK, CHUNK)
+        deliver(1, 1)
+        message(2)
+        activate(1, 3 * CHUNK, CHUNK, 0)
+        activate(1, 3 * CHUNK, CHUNK, 2)
+        deliver(2, 0)
+        pack(1, 3 * CHUNK, CHUNK)
+        deliver(2, 1)
+        message(3)
+        deliver(3, 0)
+        deliver(3, 1)
+        scatter(PACK - 1, 0, J)
+
+        out_rows = out_0.rearrange("(p t) c -> p t c", t=PACK)
+        quarters = T // QUARTER
+        pairs = [
+            ring.tile([P, 2, QUARTER, 2], BF16, name="pairs%d" % q, tag="big", bufs=6, align_bytes=64)
+            for q in range(quarters)
+        ]
+        for t in range(PACK):
+            nc.sync.dma_start(out=out_rows[:, t, :], in_=pages[t][:])
+            for q in range(quarters):
+                nc.scalar.copy(pairs[q][:, t // 2, :, t % 2], pages[t][:, q * QUARTER : (q + 1) * QUARTER])
+        o_scales = keep.tile([P, T], U8, name="o_scales", align_bytes=64)
+        out_words = out_1[0].rearrange("p c i -> p (c i)").bitcast(I32)
+        o_bf = {}
+
+        def weave(q):
+            o_bf[q] = ring.tile([P, PACK * QUARTER], BF16, name="o_bf", tag="qin", bufs=3, align_bytes=64)
+            nc.vector.tensor_copy(
+                o_bf[q][:].bitcast(I32).rearrange("p (c k u) -> p c u k", k=2, u=2),
+                pairs[q][:].rearrange("p u c e -> p (u c e)").bitcast(I32).rearrange("p (u c k) -> p c u k", u=2, k=2),
+            )
+
+        weave(0)
+        for q in range(quarters):
+            if q + 1 < quarters:
+                weave(q + 1)
+            cols = slice(q * QUARTER, (q + 1) * QUARTER)
+            o_codes = keep.tile([P, QUARTER], U32, name="o_codes%d" % q, align_bytes=64)
+            nc.vector.quantize_mx(out=o_codes[:].bitcast(FP8X4), scales=o_scales[:, cols], in_=o_bf[q][:])
+            nc.sync.dma_start(out=out_words[:, cols], in_=o_codes[:].bitcast(I32))
+        for q in range(4):
+            nc.scalar.dma_start(
+                out=out_2[0, 4 * q : 4 * q + 4, :].bitcast(I32), in_=o_scales[32 * q : 32 * q + 4, :].bitcast(I32)
+            )

@@ -22,7 +22,7 @@ PASS = P * PACK
 BANK = 512
 CHUNK = 256
 QUARTER = 512
-SCALAR_CASTS = 6
+SCALAR_CASTS = 4
 HALF = J // 2
 
 
@@ -76,41 +76,37 @@ def tile_list_msg_silu_gateP_kernel(
         nc.sync.dma_start(out=sm_sb[:], in_=sm.rearrange("(b p t) -> p b t", p=P, t=PACK))
         load_tab(0, 4)
         load_scale_rows(nc.sync, tab_sc, tab_scales)
-        load_piece(0, 2)
-        load_tab(1, 4)
+        load_piece(0)
         load_piece(1)
+        load_tab(1, 1)
         load_piece(2)
         load_piece(3)
         load_piece(4)
-        wd_raw = keep.tile([P, 2, N], I32, name="wd_raw", align_bytes=64)
-        nc.sync.dma_start(out=wd_raw[:], in_=wd_words.rearrange("a p n i -> p a (n i)").bitcast(I32))
-        load_scale_rows(nc.sync, wd_sc_raw, wd_scales)
+        load_piece(5)
 
         pages = [keep.tile([P, T], F32, name="page%d" % t) for t in range(PACK)]
         for t in range(PACK):
-            nc.vector.memset(pages[t][:], 0.0)
+            nc.vector.memset(pages[t][:].bitcast(I32), 0)
 
         v_words = {}
         v_scales = {}
 
-        def gather_words(a, half, tag):
-            v_words[a, half] = ring.tile([P, 2, HALF], U32, name="v_words", tag=tag, bufs=1, align_bytes=64)
+        def gather_words(a):
             for side in range(2):
-                entries = lists[side][:, half * HALF // 16 : (half + 1) * HALF // 16]
-                nc.vector.tensor_copy(v_words[a, half][:, side, :], tab_w[a][:].bitcast(U32).indirect(entries))
+                v_words[side, a] = keep.tile([P, J], U32, name="v_words%d%d" % (side, a), align_bytes=64)
+                nc.vector.tensor_copy(v_words[side, a][:], tab_w[a][:].bitcast(U32).indirect(lists[side][:]))
 
-        def gather_scales(half, tag):
-            v_scales[half] = ring.tile([P, 2, HALF], U8, name="v_scales", tag=tag, bufs=1, align_bytes=64)
+        def gather_scales():
             for side in range(2):
-                entries = lists[side][:, half * HALF // 16 : (half + 1) * HALF // 16]
-                nc.vector.tensor_copy(v_scales[half][:, side, :], tab_sc[:].indirect(entries))
+                v_scales[side] = keep.tile([P, J], U8, name="v_scales%d" % side, align_bytes=64)
+                nc.vector.tensor_copy(v_scales[side][:], tab_sc[:].indirect(lists[side][:]))
 
         w_codes = {}
         w_scales = {}
         w_bf = {}
 
-        def cast_piece(n, tag="qin", bufs=3):
-            w_bf[n] = ring.tile([P, PACK * PASS], BF16, name="w_bf", tag=tag, bufs=bufs, align_bytes=64)
+        def cast_piece(n):
+            w_bf[n] = ring.tile([P, PACK * PASS], BF16, name="w_bf", tag="qin%d" % (0, 1, 2, 3, 3, 0, 1, 2)[n], bufs=1, align_bytes=64)
             dst = w_bf[n][:].rearrange("p (t m i) -> p m i t", t=PACK, i=PACK)
             src = raw[n][:].rearrange("p i (m t) -> p m i t", t=PACK)
             if n < SCALAR_CASTS:
@@ -123,21 +119,27 @@ def tile_list_msg_silu_gateP_kernel(
             w_scales[n] = keep.tile([P, PASS], U8, name="w_scales%d" % n, align_bytes=64)
             nc.vector.quantize_mx(out=w_codes[n][:].bitcast(FP8X4), scales=w_scales[n][:], in_=w_bf[n][:])
 
-        gather_words(0, 0, "words00")
-        gather_words(0, 1, "words01")
-        gather_scales(0, "scales0")
-        gather_words(1, 0, "words10")
+        gather_words(0)
+        gather_scales()
         for n in range(2):
             cast_piece(n)
             quant_piece(n)
-        cast_piece(2, "words11", 1)
-        quant_piece(2)
-        gather_words(1, 1, "words11")
-        cast_piece(3, "scales1", 1)
-        quant_piece(3)
-        gather_scales(1, "scales1")
+        gather_words(1)
+        for n in range(2, 4):
+            cast_piece(n)
+            quant_piece(n)
+        load_piece(6)
+        load_piece(7)
+        wd_raw = ring.tile([P, 2, N], I32, name="wd_raw", tag="big", bufs=6, align_bytes=64)
+        nc.sync.dma_start(out=wd_raw[:], in_=wd_words.rearrange("a p n i -> p a (n i)").bitcast(I32))
+        load_scale_rows(nc.sync, wd_sc_raw, wd_scales)
+        wgo_sb = ring.tile([P, J], F32, name="wgo_sb", tag="big", bufs=6, align_bytes=64)
+        nc.sync.dma_start(out=wgo_sb[:], in_=wgo)
         cast_piece(4)
-        quant_piece(4)
+        for n in range(4, 8):
+            if n + 1 < 8:
+                cast_piece(n + 1)
+            quant_piece(n)
 
         wd_w = keep.tile([P, 2, N], I32, name="wd_w", align_bytes=64)
         wd_sc = keep.tile([P, N], U8, name="wd_sc", align_bytes=64)
@@ -147,14 +149,6 @@ def tile_list_msg_silu_gateP_kernel(
         nc.vector.tensor_copy(
             wd_sc[:].rearrange("p (t m) -> p t m", t=PACK), wd_sc_raw[:].rearrange("p (m t) -> p t m", t=PACK)
         )
-
-        for n in range(5, 8):
-            load_piece(n)
-        wgo_sb = keep.tile([P, J], F32, name="wgo_sb")
-        nc.sync.dma_start(out=wgo_sb[:], in_=wgo)
-        for n in range(5, 8):
-            cast_piece(n)
-            quant_piece(n)
 
         g_rows = {}
         gates = {}
@@ -166,7 +160,7 @@ def tile_list_msg_silu_gateP_kernel(
         for t in range(PACK):
             g_rows[t] = ring.tile([P, T], F32, name="g_rows", tag="big", bufs=6, align_bytes=64)
             nc.sync.dma_start(out=g_rows[t][:], in_=gT.rearrange("(p t) c -> p t c", t=PACK)[:, t, :])
-        for t in range(PACK - 1):
+        for t in range(2):
             gate(t, "gate%d" % t)
 
         h_codes = [keep.tile([P, J], U32, name="h_codes%d" % b, align_bytes=64) for b in range(2)]
@@ -174,13 +168,12 @@ def tile_list_msg_silu_gateP_kernel(
 
         h_rows = {}
 
-        def activate(b, j0, width, t0):
-            half = j0 // HALF
-            cols = slice(j0 % HALF, j0 % HALF + width)
+        def activate(b, j0, width, t0, act_tag="act", act_bufs=2):
+            cols = slice(j0, j0 + width)
             per_bank = BANK // width
             if t0 == 0:
-                h_rows[b, j0] = ring.tile([P, PACK, width], BF16, name="h_rows", tag="h_rows", bufs=1)
-            bank = psum.tile([P, per_bank, width], F32, name="a_bank", tag="a")
+                h_rows[b, j0] = ring.tile([P, PACK, width], BF16, name="h_rows", tag="rows%d_%d" % (b, j0), bufs=1)
+            bank = psum.tile([P, per_bank, width], F32, name="a_bank", tag="a", bufs=7)
             for u in range(per_bank):
                 rows = slice((t0 + u) * P, (t0 + u + 1) * P)
                 for s in range(4):
@@ -190,97 +183,102 @@ def tile_list_msg_silu_gateP_kernel(
                         out=bank[:, u, :],
                         lhsT=w_codes[n][:, rows].bitcast(FP8X4),
                         lhsT_scale=w_scales[n][:, rows],
-                        rhs=v_words[a, half][:, side, cols].bitcast(FP8X4),
-                        rhs_scale=v_scales[half][4 * a : P, side, cols],
+                        rhs=v_words[side, a][:, cols].bitcast(FP8X4),
+                        rhs_scale=v_scales[side][4 * a : P, cols],
                         start=(s == 0),
                         stop=(s == 3),
                     )
-            act = ring.tile([P, per_bank, width], F32, name="act", tag="act", bufs=2)
+            act = ring.tile([P, per_bank, width], F32, name="act", tag=act_tag, bufs=act_bufs)
             nc.scalar.activation(act[:], bank[:], SILU)
             for u in range(per_bank):
                 t = t0 + u
                 nc.scalar.activation(h_rows[b, j0][:, t, :], act[:, u, :], COPY, scale=sm_sb[:, b, t : t + 1])
 
-        def pack(b, j0, width, tag="qin", bufs=3):
+        def pack(b, j0, width, tag):
             cols = slice(j0, j0 + width)
-            h_bf = ring.tile([P, PACK * width], BF16, name="h_bf", tag=tag, bufs=bufs, align_bytes=64)
+            h_bf = ring.tile([P, PACK * width], BF16, name="h_bf", tag=tag, bufs=1, align_bytes=64)
             nc.scalar.copy(
                 h_bf[:].rearrange("p (c i t) -> p c t i", i=4, t=PACK),
                 h_rows[b, j0][:].rearrange("p t (c i) -> p c t i", i=4),
             )
             nc.vector.quantize_mx(out=h_codes[b][:, cols].bitcast(FP8X4), scales=h_scales[b][:, cols], in_=h_bf[:])
 
-        def hidden(b, j0, width):
-            for t0 in range(0, PACK, BANK // width):
-                activate(b, j0, width, t0)
-            pack(b, j0, width)
+        y_last = keep.tile([P, J], F32, name="y_last")
 
-        y_sb = [keep.tile([P, 2, J], F32, name="y_sb%d" % u) for u in range(2)]
-        y_banks = {}
-
-        def message(c):
+        def message(c, u, tag="y", bufs=1):
             cols = slice(c * CHUNK, (c + 1) * CHUNK)
-            for u in range(2):
-                bank = psum.tile([P, 2, CHUNK], F32, name="y_bank", tag="y")
-                y_banks[c, u] = bank
-                for e in range(2):
-                    t = 2 * u + e
-                    rows = slice(t * P, (t + 1) * P)
-                    for b in range(2):
-                        nc.tensor.matmul_mx(
-                            out=bank[:, e, :],
-                            lhsT=wd_w[:, b, rows].bitcast(FP8X4),
-                            lhsT_scale=wd_sc[4 * b : P, rows],
-                            rhs=h_codes[b][:, cols].bitcast(FP8X4),
-                            rhs_scale=h_scales[b][:, cols],
-                            start=(b == 0),
-                            stop=(b == 1),
-                        )
+            bank = psum.tile([P, 2, CHUNK], F32, name="y_bank", tag=tag, bufs=bufs)
+            for e in range(2):
+                rows = slice((2 * u + e) * P, (2 * u + e + 1) * P)
+                for b in range(2):
+                    nc.tensor.matmul_mx(
+                        out=bank[:, e, :],
+                        lhsT=wd_w[:, b, rows].bitcast(FP8X4),
+                        lhsT_scale=wd_sc[4 * b : P, rows],
+                        rhs=h_codes[b][:, cols].bitcast(FP8X4),
+                        rhs_scale=h_scales[b][:, cols],
+                        start=(b == 0),
+                        stop=(b == 1),
+                    )
+            return bank
 
-        def scatter(t, j0, width):
-            cols = slice(j0, j0 + width)
+        def scatter(t, y, j0, width):
             nc.vector.tensor_tensor(
                 pages[t][:].indirect(dst_list[:, j0 // 16 : (j0 + width) // 16]),
-                y_sb[t // 2][:, t % 2, cols],
-                gates[t][:, cols],
+                y,
+                gates[t][:, j0 : j0 + width],
                 MULT,
             )
 
-        def deliver(c, u):
-            cols = slice(c * CHUNK, (c + 1) * CHUNK)
-            nc.scalar.copy(y_sb[u][:, :, cols], y_banks[c, u][:])
-            for t in (2 * u, 2 * u + 1):
-                if t < PACK - 1:
-                    scatter(t, c * CHUNK, CHUNK)
+        def deliver_low(c, tag):
+            bank = message(c, 0)
+            y = ring.tile([P, 2, CHUNK], F32, name="y_low", tag=tag, bufs=1)
+            nc.scalar.copy(y[:], bank[:])
+            for t in range(2):
+                scatter(t, y[:, t, :], c * CHUNK, CHUNK)
 
-        hidden(0, 0, 512)
-        hidden(1, 0, CHUNK)
+        def deliver_high(c, y, tag="y", bufs=1):
+            bank = message(c, 1, tag, bufs)
+            nc.scalar.copy(y, bank[:, 0, :])
+            nc.scalar.copy(y_last[:, c * CHUNK : (c + 1) * CHUNK], bank[:, 1, :])
+
+        for t in range(PACK):
+            activate(0, 0, HALF, t)
+        pack(0, 0, HALF, "qin3")
+        activate(1, 0, CHUNK, 0)
+        activate(1, 0, CHUNK, 2)
+        pack(1, 0, CHUNK, "gate2")
+        gate(2, "gate2")
         activate(1, CHUNK, CHUNK, 0)
         activate(1, CHUNK, CHUNK, 2)
-        message(0)
-        deliver(0, 0)
-        pack(1, CHUNK, CHUNK)
-        deliver(0, 1)
-        message(1)
-        activate(0, 512, 512, 0)
-        activate(0, 512, 512, 1)
-        activate(0, 512, 512, 2)
-        deliver(1, 0)
-        activate(0, 512, 512, 3)
-        pack(0, 512, 512, "gate3", 1)
-        gate(3, "gate3")
-        hidden(1, 2 * CHUNK, CHUNK)
-        deliver(1, 1)
-        message(2)
+        pack(1, CHUNK, CHUNK, "qin0")
+        deliver_low(0, "rows1_256")
+        y0 = ring.tile([P, CHUNK], F32, name="y_high0", tag="y_high0", bufs=1)
+        deliver_high(0, y0[:])
+        scatter(2, y0[:], 0, CHUNK)
+        activate(0, HALF, HALF, 0)
+        activate(0, HALF, HALF, 1)
+        activate(0, HALF, HALF, 2, "act_y", 1)
+        deliver_low(1, "act_y")
+        activate(0, HALF, HALF, 3)
+        pack(0, HALF, HALF, "qin1")
+        activate(1, 2 * CHUNK, CHUNK, 0)
+        activate(1, 2 * CHUNK, CHUNK, 2)
+        pack(1, 2 * CHUNK, CHUNK, "qin2")
+        y1 = ring.tile([P, CHUNK], F32, name="y_high1", tag="rows1_512", bufs=1)
+        deliver_high(1, y1[:])
+        scatter(2, y1[:], CHUNK, CHUNK)
         activate(1, 3 * CHUNK, CHUNK, 0)
         activate(1, 3 * CHUNK, CHUNK, 2)
-        deliver(2, 0)
-        pack(1, 3 * CHUNK, CHUNK)
-        deliver(2, 1)
-        message(3)
-        deliver(3, 0)
-        deliver(3, 1)
-        scatter(PACK - 1, 0, J)
+        deliver_low(2, "y_low2")
+        pack(1, 3 * CHUNK, CHUNK, "gate3")
+        gate(3, "gate3")
+        y23 = ring.tile([P, HALF], F32, name="y_high23", tag="rows1_768", bufs=1)
+        deliver_high(2, y23[:, 0:CHUNK])
+        deliver_low(3, "y_low3")
+        deliver_high(3, y23[:, CHUNK:HALF], "a", 7)
+        scatter(2, y23[:], HALF, HALF)
+        scatter(PACK - 1, y_last[:], 0, J)
 
         out_rows = out_0.rearrange("(p t) c -> p t c", t=PACK)
         quarters = T // QUARTER
@@ -292,16 +290,18 @@ def tile_list_msg_silu_gateP_kernel(
             nc.sync.dma_start(out=out_rows[:, t, :], in_=pages[t][:])
             for q in range(quarters):
                 nc.scalar.copy(pairs[q][:, t // 2, :, t % 2], pages[t][:, q * QUARTER : (q + 1) * QUARTER])
-        o_scales = keep.tile([P, T], U8, name="o_scales", align_bytes=64)
+        o_scales = keep.tile([P, QUARTER], U8, name="o_scales", align_bytes=64)
         out_words = out_1[0].rearrange("p c i -> p (c i)").bitcast(I32)
         o_bf = {}
 
         def weave(q):
-            o_bf[q] = ring.tile([P, PACK * QUARTER], BF16, name="o_bf", tag="qin", bufs=3, align_bytes=64)
-            nc.vector.tensor_copy(
-                o_bf[q][:].bitcast(I32).rearrange("p (c k u) -> p c u k", k=2, u=2),
-                pairs[q][:].rearrange("p u c e -> p (u c e)").bitcast(I32).rearrange("p (u c k) -> p c u k", u=2, k=2),
-            )
+            o_bf[q] = ring.tile([P, PACK * QUARTER], BF16, name="o_bf", tag="qin%d" % q, bufs=1, align_bytes=64)
+            dst = o_bf[q][:].bitcast(F32).rearrange("p (c k u) -> p c u k", k=2, u=2)
+            src = pairs[q][:].rearrange("p u c e -> p (u c e)").bitcast(F32).rearrange("p (u c k) -> p c u k", u=2, k=2)
+            if q + 1 < quarters:
+                nc.vector.tensor_copy(dst, src)
+            else:
+                nc.scalar.copy(dst, src)
 
         weave(0)
         for q in range(quarters):
@@ -309,9 +309,10 @@ def tile_list_msg_silu_gateP_kernel(
                 weave(q + 1)
             cols = slice(q * QUARTER, (q + 1) * QUARTER)
             o_codes = keep.tile([P, QUARTER], U32, name="o_codes%d" % q, align_bytes=64)
-            nc.vector.quantize_mx(out=o_codes[:].bitcast(FP8X4), scales=o_scales[:, cols], in_=o_bf[q][:])
+            nc.vector.quantize_mx(out=o_codes[:].bitcast(FP8X4), scales=o_scales[4 * q : P, :], in_=o_bf[q][:])
             nc.sync.dma_start(out=out_words[:, cols], in_=o_codes[:].bitcast(I32))
         for q in range(4):
             nc.scalar.dma_start(
-                out=out_2[0, 4 * q : 4 * q + 4, :].bitcast(I32), in_=o_scales[32 * q : 32 * q + 4, :].bitcast(I32)
+                out=out_2[0, 4 * q : 4 * q + 4, :].bitcast(I32).rearrange("r (g c) -> g r c", g=quarters),
+                in_=o_scales[32 * q : 32 * q + 16, :].bitcast(I32),
             )

@@ -63,14 +63,12 @@ def tile_list_msg_silu_gateP_kernel(
         pieces = [(b, side, a) for b in range(2) for a in range(2) for side in range(2)]
         raw = {}
 
-        def load_piece(n, parts=1):
+        def load_piece(n):
             b, side, a = pieces[n]
             w = (ws, wt)[side]
-            raw[n] = ring.tile([P, PACK, PASS], F32, name="w_raw", tag="big", bufs=6, align_bytes=64)
+            raw[n] = ring.tile([P, PACK, PASS], F32, name="w_raw", tag="big%d" % (0, 1, 2, 3, 4, 5, 1, 2)[n], bufs=1, align_bytes=64)
             rows = w[a * PASS : (a + 1) * PASS, b * PASS : (b + 1) * PASS].rearrange("(p i) c -> p i c", i=PACK)
-            for q in range(parts):
-                slots = slice(q * PACK // parts, (q + 1) * PACK // parts)
-                nc.sync.dma_start(out=raw[n][:, slots, :], in_=rows[:, slots, :])
+            nc.sync.dma_start(out=raw[n][:], in_=rows)
 
         sm_sb = keep.tile([P, 2, PACK], F32, name="sm_sb")
         nc.sync.dma_start(out=sm_sb[:], in_=sm.rearrange("(b p t) -> p b t", p=P, t=PACK))
@@ -83,6 +81,8 @@ def tile_list_msg_silu_gateP_kernel(
         load_piece(3)
         load_piece(4)
         load_piece(5)
+        wgo_sb = keep.tile([P, J], F32, name="wgo_sb")
+        nc.sync.dma_start(out=wgo_sb[:], in_=wgo)
 
         pages = [keep.tile([P, T], F32, name="page%d" % t) for t in range(PACK)]
         for t in range(PACK):
@@ -91,10 +91,9 @@ def tile_list_msg_silu_gateP_kernel(
         v_words = {}
         v_scales = {}
 
-        def gather_words(a):
-            for side in range(2):
-                v_words[side, a] = keep.tile([P, J], U32, name="v_words%d%d" % (side, a), align_bytes=64)
-                nc.vector.tensor_copy(v_words[side, a][:], tab_w[a][:].bitcast(U32).indirect(lists[side][:]))
+        def gather_words(side, a):
+            v_words[side, a] = ring.tile([P, J], U32, name="v_words", tag="words%d%d" % (side, a), bufs=1, align_bytes=64)
+            nc.vector.tensor_copy(v_words[side, a][:], tab_w[a][:].bitcast(U32).indirect(lists[side][:]))
 
         def gather_scales():
             for side in range(2):
@@ -106,7 +105,7 @@ def tile_list_msg_silu_gateP_kernel(
         w_bf = {}
 
         def cast_piece(n):
-            w_bf[n] = ring.tile([P, PACK * PASS], BF16, name="w_bf", tag="qin%d" % (0, 1, 2, 3, 3, 0, 1, 2)[n], bufs=1, align_bytes=64)
+            w_bf[n] = ring.tile([P, PACK * PASS], BF16, name="w_bf", tag=("qin0", "qin1", "words11", "qin3", "qin3", "qin0", "qin1", "qin2")[n], bufs=1, align_bytes=64)
             dst = w_bf[n][:].rearrange("p (t m i) -> p m i t", t=PACK, i=PACK)
             src = raw[n][:].rearrange("p i (m t) -> p m i t", t=PACK)
             if n < SCALAR_CASTS:
@@ -119,27 +118,47 @@ def tile_list_msg_silu_gateP_kernel(
             w_scales[n] = keep.tile([P, PASS], U8, name="w_scales%d" % n, align_bytes=64)
             nc.vector.quantize_mx(out=w_codes[n][:].bitcast(FP8X4), scales=w_scales[n][:], in_=w_bf[n][:])
 
-        gather_words(0)
+        gather_words(0, 0)
+        gather_words(1, 0)
         gather_scales()
         for n in range(2):
             cast_piece(n)
             quant_piece(n)
-        gather_words(1)
-        for n in range(2, 4):
-            cast_piece(n)
-            quant_piece(n)
+        gather_words(0, 1)
+        cast_piece(2)
+        quant_piece(2)
+        gather_words(1, 1)
+        cast_piece(3)
+        quant_piece(3)
+        g_rows = {}
+        gates = {}
+
+        def load_gate_rows(t, tag):
+            g_rows[t] = ring.tile([P, T], F32, name="g_rows", tag=tag, bufs=1, align_bytes=64)
+            nc.sync.dma_start(out=g_rows[t][:], in_=gT.rearrange("(p t) c -> p t c", t=PACK)[:, t, :])
+
+        def gate(t, tag):
+            gates[t] = ring.tile([P, J], F32, name="gate", tag=tag, bufs=1, align_bytes=64)
+            nc.vector.tensor_tensor(gates[t][:], g_rows[t][:].indirect(src_list[:]), wgo_sb[:], MULT)
+
+        load_gate_rows(2, "big0")
         load_piece(6)
         load_piece(7)
-        wd_raw = ring.tile([P, 2, N], I32, name="wd_raw", tag="big", bufs=6, align_bytes=64)
+        wd_raw = ring.tile([P, 2, N], I32, name="wd_raw", tag="big3", bufs=1, align_bytes=64)
         nc.sync.dma_start(out=wd_raw[:], in_=wd_words.rearrange("a p n i -> p a (n i)").bitcast(I32))
         load_scale_rows(nc.sync, wd_sc_raw, wd_scales)
-        wgo_sb = ring.tile([P, J], F32, name="wgo_sb", tag="big", bufs=6, align_bytes=64)
-        nc.sync.dma_start(out=wgo_sb[:], in_=wgo)
         cast_piece(4)
-        for n in range(4, 8):
-            if n + 1 < 8:
-                cast_piece(n + 1)
-            quant_piece(n)
+        cast_piece(5)
+        quant_piece(4)
+        quant_piece(5)
+        load_gate_rows(3, "big4")
+        load_gate_rows(1, "big5")
+        gate(2, "gate2")
+        load_gate_rows(0, "big0")
+        cast_piece(6)
+        cast_piece(7)
+        quant_piece(6)
+        quant_piece(7)
 
         wd_w = keep.tile([P, 2, N], I32, name="wd_w", align_bytes=64)
         wd_sc = keep.tile([P, N], U8, name="wd_sc", align_bytes=64)
@@ -150,73 +169,62 @@ def tile_list_msg_silu_gateP_kernel(
             wd_sc[:].rearrange("p (t m) -> p t m", t=PACK), wd_sc_raw[:].rearrange("p (m t) -> p t m", t=PACK)
         )
 
-        g_rows = {}
-        gates = {}
-
-        def gate(t, tag):
-            gates[t] = ring.tile([P, J], F32, name="gate", tag=tag, bufs=1, align_bytes=64)
-            nc.vector.tensor_tensor(gates[t][:], g_rows[t][:].indirect(src_list[:]), wgo_sb[:], MULT)
-
-        for t in range(PACK):
-            g_rows[t] = ring.tile([P, T], F32, name="g_rows", tag="big", bufs=6, align_bytes=64)
-            nc.sync.dma_start(out=g_rows[t][:], in_=gT.rearrange("(p t) c -> p t c", t=PACK)[:, t, :])
-        for t in range(2):
-            gate(t, "gate%d" % t)
-
-        h_codes = [keep.tile([P, J], U32, name="h_codes%d" % b, align_bytes=64) for b in range(2)]
-        h_scales = [keep.tile([P, J], U8, name="h_scales%d" % b, align_bytes=64) for b in range(2)]
-
+        h_codes = {}
+        h_scales = {}
         h_rows = {}
+        per_bank_bufs = (4, 2)
 
-        def activate(b, j0, width, t0, act_tag="act", act_bufs=2):
+        def activate(b, j0, width, t0):
             cols = slice(j0, j0 + width)
             per_bank = BANK // width
             if t0 == 0:
-                h_rows[b, j0] = ring.tile([P, PACK, width], BF16, name="h_rows", tag="rows%d_%d" % (b, j0), bufs=1)
-            bank = psum.tile([P, per_bank, width], F32, name="a_bank", tag="a", bufs=7)
-            for u in range(per_bank):
-                rows = slice((t0 + u) * P, (t0 + u + 1) * P)
-                for s in range(4):
-                    n = 4 * b + s
-                    side, a = pieces[n][1:]
+                h_rows[b, j0] = ring.tile([P, PACK, width], BF16, name="h_rows", tag="rows%d_%d" % (b, j0), bufs=1, align_bytes=64)
+            bank = psum.tile([P, per_bank, width], F32, name="a_bank", tag="a%d" % b, bufs=per_bank_bufs[b])
+            for s in range(4):
+                n = 4 * b + s
+                side, a = pieces[n][1:]
+                for u in range(per_bank):
+                    rows = slice((t0 + u) * P, (t0 + u + 1) * P)
                     nc.tensor.matmul_mx(
                         out=bank[:, u, :],
                         lhsT=w_codes[n][:, rows].bitcast(FP8X4),
                         lhsT_scale=w_scales[n][:, rows],
                         rhs=v_words[side, a][:, cols].bitcast(FP8X4),
                         rhs_scale=v_scales[side][4 * a : P, cols],
-                        start=(s == 0),
-                        stop=(s == 3),
+                        start=(s == 0 and u == 0),
+                        stop=(s == 3 and u == per_bank - 1),
                     )
-            act = ring.tile([P, per_bank, width], F32, name="act", tag=act_tag, bufs=act_bufs)
+            act = ring.tile([P, per_bank, width], F32, name="act", tag="act", bufs=2)
             nc.scalar.activation(act[:], bank[:], SILU)
             for u in range(per_bank):
                 t = t0 + u
                 nc.scalar.activation(h_rows[b, j0][:, t, :], act[:, u, :], COPY, scale=sm_sb[:, b, t : t + 1])
 
-        def pack(b, j0, width, tag):
-            cols = slice(j0, j0 + width)
+        def pack(b, j0, width, tag, codes_tag):
             h_bf = ring.tile([P, PACK * width], BF16, name="h_bf", tag=tag, bufs=1, align_bytes=64)
             nc.scalar.copy(
                 h_bf[:].rearrange("p (c i t) -> p c t i", i=4, t=PACK),
                 h_rows[b, j0][:].rearrange("p t (c i) -> p c t i", i=4),
             )
-            nc.vector.quantize_mx(out=h_codes[b][:, cols].bitcast(FP8X4), scales=h_scales[b][:, cols], in_=h_bf[:])
+            h_codes[b, j0] = ring.tile([P, width], U32, name="h_codes", tag=codes_tag, bufs=1, align_bytes=64)
+            h_scales[b, j0] = keep.tile([P, width], U8, name="h_scales%d_%d" % (b, j0), align_bytes=64)
+            nc.vector.quantize_mx(out=h_codes[b, j0][:].bitcast(FP8X4), scales=h_scales[b, j0][:], in_=h_bf[:])
 
         y_last = keep.tile([P, J], F32, name="y_last")
 
         def message(c, u, tag="y", bufs=1):
-            cols = slice(c * CHUNK, (c + 1) * CHUNK)
             bank = psum.tile([P, 2, CHUNK], F32, name="y_bank", tag=tag, bufs=bufs)
             for e in range(2):
                 rows = slice((2 * u + e) * P, (2 * u + e + 1) * P)
                 for b in range(2):
+                    j0 = c * CHUNK if b else c * CHUNK // HALF * HALF
+                    cols = slice(c * CHUNK - j0, (c + 1) * CHUNK - j0)
                     nc.tensor.matmul_mx(
                         out=bank[:, e, :],
                         lhsT=wd_w[:, b, rows].bitcast(FP8X4),
                         lhsT_scale=wd_sc[4 * b : P, rows],
-                        rhs=h_codes[b][:, cols].bitcast(FP8X4),
-                        rhs_scale=h_scales[b][:, cols],
+                        rhs=h_codes[b, j0][:, cols].bitcast(FP8X4),
+                        rhs_scale=h_scales[b, j0][:, cols],
                         start=(b == 0),
                         stop=(b == 1),
                     )
@@ -230,60 +238,71 @@ def tile_list_msg_silu_gateP_kernel(
                 MULT,
             )
 
-        def deliver_low(c, tag):
-            bank = message(c, 0)
-            y = ring.tile([P, 2, CHUNK], F32, name="y_low", tag=tag, bufs=1)
+        def y_tile(shape, tag):
+            return ring.tile(shape, F32, name="y_" + tag, tag=tag, bufs=1, align_bytes=64)
+
+        def deliver(t, c, bank, tag):
+            y = y_tile([P, CHUNK], tag)
+            nc.scalar.copy(y[:], bank[:, t % 2, :])
+            scatter(t, y[:], c * CHUNK, CHUNK)
+
+        def deliver_low(c, tag, bank_tag="y", bank_bufs=1):
+            bank = message(c, 0, bank_tag, bank_bufs)
+            y = y_tile([P, 2, CHUNK], tag)
             nc.scalar.copy(y[:], bank[:])
             for t in range(2):
                 scatter(t, y[:, t, :], c * CHUNK, CHUNK)
 
-        def deliver_high(c, y, tag="y", bufs=1):
-            bank = message(c, 1, tag, bufs)
+        def deliver_high(c, y):
+            bank = message(c, 1)
             nc.scalar.copy(y, bank[:, 0, :])
             nc.scalar.copy(y_last[:, c * CHUNK : (c + 1) * CHUNK], bank[:, 1, :])
 
         for t in range(PACK):
             activate(0, 0, HALF, t)
-        pack(0, 0, HALF, "qin3")
+        pack(0, 0, HALF, "qin3", "qin2")
+        gate(3, "gate3")
+        gate(1, "gate1")
+        for t in range(PACK):
+            activate(0, HALF, HALF, t)
         activate(1, 0, CHUNK, 0)
         activate(1, 0, CHUNK, 2)
-        pack(1, 0, CHUNK, "gate2")
-        gate(2, "gate2")
+        pack(1, 0, CHUNK, "gate0", "big5")
+        gate(0, "gate0")
+        bank = message(0, 0)
+        deliver(0, 0, bank, "low0")
+        pack(0, HALF, HALF, "rows1_0", "low0")
+        deliver(1, 0, bank, "big0")
         activate(1, CHUNK, CHUNK, 0)
         activate(1, CHUNK, CHUNK, 2)
-        pack(1, CHUNK, CHUNK, "qin0")
-        deliver_low(0, "rows1_256")
-        y0 = ring.tile([P, CHUNK], F32, name="y_high0", tag="y_high0", bufs=1)
-        deliver_high(0, y0[:])
-        scatter(2, y0[:], 0, CHUNK)
-        activate(0, HALF, HALF, 0)
-        activate(0, HALF, HALF, 1)
-        activate(0, HALF, HALF, 2, "act_y", 1)
-        deliver_low(1, "act_y")
-        activate(0, HALF, HALF, 3)
-        pack(0, HALF, HALF, "qin1")
+        pack(1, CHUNK, CHUNK, "qin0", "big0")
+        y02 = y_tile([P, CHUNK], "rows1_256")
+        deliver_high(0, y02[:])
+        scatter(2, y02[:], 0, CHUNK)
+        deliver_low(1, "low1")
         activate(1, 2 * CHUNK, CHUNK, 0)
         activate(1, 2 * CHUNK, CHUNK, 2)
-        pack(1, 2 * CHUNK, CHUNK, "qin2")
-        y1 = ring.tile([P, CHUNK], F32, name="y_high1", tag="rows1_512", bufs=1)
-        deliver_high(1, y1[:])
-        scatter(2, y1[:], CHUNK, CHUNK)
+        pack(1, 2 * CHUNK, CHUNK, "qin1", "low1")
+        y12 = y_tile([P, CHUNK], "rows1_512")
+        deliver_high(1, y12[:])
+        scatter(2, y12[:], CHUNK, CHUNK)
         activate(1, 3 * CHUNK, CHUNK, 0)
         activate(1, 3 * CHUNK, CHUNK, 2)
-        deliver_low(2, "y_low2")
-        pack(1, 3 * CHUNK, CHUNK, "gate3")
-        gate(3, "gate3")
-        y23 = ring.tile([P, HALF], F32, name="y_high23", tag="rows1_768", bufs=1)
+        bank = message(2, 0)
+        deliver(0, 2, bank, "low2")
+        pack(1, 3 * CHUNK, CHUNK, "qin3", "low2")
+        deliver(1, 2, bank, "rows1_768")
+        y23 = y_tile([P, HALF], "high23")
+        deliver_low(3, "low3", "a0", 4)
         deliver_high(2, y23[:, 0:CHUNK])
-        deliver_low(3, "y_low3")
-        deliver_high(3, y23[:, CHUNK:HALF], "a", 7)
+        deliver_high(3, y23[:, CHUNK:HALF])
         scatter(2, y23[:], HALF, HALF)
         scatter(PACK - 1, y_last[:], 0, J)
 
         out_rows = out_0.rearrange("(p t) c -> p t c", t=PACK)
         quarters = T // QUARTER
         pairs = [
-            ring.tile([P, 2, QUARTER, 2], BF16, name="pairs%d" % q, tag="big", bufs=6, align_bytes=64)
+            ring.tile([P, 2, QUARTER, 2], BF16, name="pairs%d" % q, tag="big%d" % (q + 1), bufs=1, align_bytes=64)
             for q in range(quarters)
         ]
         for t in range(PACK):
@@ -295,7 +314,7 @@ def tile_list_msg_silu_gateP_kernel(
         o_bf = {}
 
         def weave(q):
-            o_bf[q] = ring.tile([P, PACK * QUARTER], BF16, name="o_bf", tag="qin%d" % q, bufs=1, align_bytes=64)
+            o_bf[q] = ring.tile([P, PACK * QUARTER], BF16, name="o_bf", tag="qin%d" % (0, 1, 3, 2)[q], bufs=1, align_bytes=64)
             dst = o_bf[q][:].bitcast(F32).rearrange("p (c k u) -> p c u k", k=2, u=2)
             src = pairs[q][:].rearrange("p u c e -> p (u c e)").bitcast(F32).rearrange("p (u c k) -> p c u k", u=2, k=2)
             if q + 1 < quarters:

@@ -1,6 +1,7 @@
 from contextlib import ExitStack
 
 import concourse.mybir as mybir
+from concourse.masks import make_identity
 
 K, R, N, T, J = 1024, 1024, 512, 2048, 1024
 FLOPS = 2 * (2 * K * R * J + R * N * J)
@@ -57,7 +58,7 @@ def tile_list_msg_silu_gateP_kernel(
         def load_tab(a, parts):
             words = tab_words[a].rearrange("p t i -> p (t i)").bitcast(I32)
             for q in range(parts):
-                cols = slice(q * T // parts, (q + 1) * T // parts)
+                cols = slice(q * T // parts // 64 * 64, (q + 1) * T // parts // 64 * 64)
                 nc.sync.dma_start(out=tab_w[a][:, cols], in_=words[:, cols])
 
         pieces = [(b, side, a) for b in range(2) for a in range(2) for side in range(2)]
@@ -72,7 +73,11 @@ def tile_list_msg_silu_gateP_kernel(
 
         sm_sb = keep.tile([P, 2, PACK], F32, name="sm_sb")
         nc.sync.dma_start(out=sm_sb[:], in_=sm.rearrange("(b p t) -> p b t", p=P, t=PACK))
-        load_tab(0, 4)
+        wgo_row = keep.tile([P, J // P], F32, name="wgo_row")
+        nc.sync.dma_start(out=wgo_row[:], in_=wgo[0].rearrange("(p e) -> p e", p=P))
+        identity = keep.tile([P, P], F32, name="identity")
+        make_identity(nc, identity[:])
+        load_tab(0, 3)
         load_scale_rows(nc.sync, tab_sc, tab_scales)
         load_piece(0)
         load_piece(1)
@@ -81,8 +86,18 @@ def tile_list_msg_silu_gateP_kernel(
         load_piece(3)
         load_piece(4)
         load_piece(5)
+        wd_raw = keep.tile([P, 2, N], I32, name="wd_raw", align_bytes=64)
+        nc.sync.dma_start(out=wd_raw[:], in_=wd_words.rearrange("a p n i -> p a (n i)").bitcast(I32))
+        load_scale_rows(nc.sync, wd_sc_raw, wd_scales)
         wgo_sb = keep.tile([P, J], F32, name="wgo_sb")
-        nc.sync.dma_start(out=wgo_sb[:], in_=wgo)
+        for half in range(2):
+            spread = psum.tile([P, PACK, P], F32, name="spread", tag="a0", bufs=4)
+            for e in range(PACK):
+                column = PACK * half + e
+                nc.tensor.transpose(spread[:, e, :], wgo_row[:, column : column + 1].to_broadcast([P, P]), identity[:])
+            nc.scalar.copy(
+                wgo_sb[:].rearrange("q (p h e) -> q h p e", h=2, e=PACK)[:, half], spread[:].rearrange("q e p -> q p e")
+            )
 
         pages = [keep.tile([P, T], F32, name="page%d" % t) for t in range(PACK)]
         for t in range(PACK):
@@ -106,8 +121,8 @@ def tile_list_msg_silu_gateP_kernel(
 
         def cast_piece(n):
             w_bf[n] = ring.tile([P, PACK * PASS], BF16, name="w_bf", tag=("qin0", "qin1", "words11", "qin3", "qin3", "qin0", "qin1", "qin2")[n], bufs=1, align_bytes=64)
-            dst = w_bf[n][:].rearrange("p (t m i) -> p m i t", t=PACK, i=PACK)
-            src = raw[n][:].rearrange("p i (m t) -> p m i t", t=PACK)
+            dst = w_bf[n][:].rearrange("p (u e m i) -> p u m i e", u=2, e=2, i=PACK)
+            src = raw[n][:].rearrange("p i (m u e) -> p u m i e", u=2, e=2)
             if n < SCALAR_CASTS:
                 nc.scalar.copy(dst, src)
             else:
@@ -144,9 +159,6 @@ def tile_list_msg_silu_gateP_kernel(
         load_gate_rows(2, "big0")
         load_piece(6)
         load_piece(7)
-        wd_raw = ring.tile([P, 2, N], I32, name="wd_raw", tag="big3", bufs=1, align_bytes=64)
-        nc.sync.dma_start(out=wd_raw[:], in_=wd_words.rearrange("a p n i -> p a (n i)").bitcast(I32))
-        load_scale_rows(nc.sync, wd_sc_raw, wd_scales)
         cast_piece(4)
         cast_piece(5)
         quant_piece(4)
@@ -163,7 +175,8 @@ def tile_list_msg_silu_gateP_kernel(
         wd_w = keep.tile([P, 2, N], I32, name="wd_w", align_bytes=64)
         wd_sc = keep.tile([P, N], U8, name="wd_sc", align_bytes=64)
         nc.vector.tensor_copy(
-            wd_w[:].rearrange("p a (t m) -> p a m t", t=PACK), wd_raw[:].rearrange("p a (m t) -> p a m t", t=PACK)
+            wd_w[:].rearrange("p a (u e m) -> p u a m e", u=2, e=2),
+            wd_raw[:].rearrange("p a (m u e) -> p u a m e", u=2, e=2),
         )
         nc.vector.tensor_copy(
             wd_sc[:].rearrange("p (t m) -> p t m", t=PACK), wd_sc_raw[:].rearrange("p (m t) -> p t m", t=PACK)
@@ -253,8 +266,8 @@ def tile_list_msg_silu_gateP_kernel(
             for t in range(2):
                 scatter(t, y[:, t, :], c * CHUNK, CHUNK)
 
-        def deliver_high(c, y):
-            bank = message(c, 1)
+        def deliver_high(c, y, bank_tag="y", bank_bufs=1):
+            bank = message(c, 1, bank_tag, bank_bufs)
             nc.scalar.copy(y, bank[:, 0, :])
             nc.scalar.copy(y_last[:, c * CHUNK : (c + 1) * CHUNK], bank[:, 1, :])
 
@@ -295,7 +308,7 @@ def tile_list_msg_silu_gateP_kernel(
         y23 = y_tile([P, HALF], "high23")
         deliver_low(3, "low3", "a0", 4)
         deliver_high(2, y23[:, 0:CHUNK])
-        deliver_high(3, y23[:, CHUNK:HALF])
+        deliver_high(3, y23[:, CHUNK:HALF], "a0", 4)
         scatter(2, y23[:], HALF, HALF)
         scatter(PACK - 1, y_last[:], 0, J)
 

@@ -23,8 +23,18 @@ PASS = P * PACK
 BANK = 512
 CHUNK = 256
 QUARTER = 512
-SCALAR_CASTS = 4
+SCALAR_CASTS = 5
 HALF = J // 2
+BIG = 8192
+QIN = 4096
+QIN_SLOTS = 5
+TAB_AT = 8 * BIG
+QIN_AT = TAB_AT + 2 * BIG
+ROWS_AT = QIN_AT + QIN_SLOTS * QIN
+ACTS = 2
+A_BANKS = 3
+ACT_AT = ROWS_AT + 2 * QIN
+CH_AT = ACT_AT + ACTS * 2048
 
 
 def tile_list_msg_silu_gateP_kernel(
@@ -33,8 +43,11 @@ def tile_list_msg_silu_gateP_kernel(
     nc = tc.nc
     with ExitStack() as ctx:
         keep = ctx.enter_context(tc.tile_pool(name="keep", bufs=1))
-        ring = ctx.enter_context(tc.tile_pool(name="ring", bufs=1))
-        psum = ctx.enter_context(tc.psum_pool(name="psum", bufs=4))
+        arena = ctx.enter_context(tc.tile_pool(name="arena", bufs=1))
+        psum = ctx.enter_context(tc.psum_pool(name="psum", bufs=1))
+
+        def placed(name, shape, dtype, offset):
+            return arena.tile(shape, dtype, name=name, align_bytes=64, offset=offset)
 
         src_list = keep.tile([P, J // 16], U16, name="src_list")
         dst_list = keep.tile([P, J // 16], U16, name="dst_list")
@@ -43,22 +56,26 @@ def tile_list_msg_silu_gateP_kernel(
         wd_sc_raw = keep.tile([P, N], U8, name="wd_sc_raw", align_bytes=64)
         nc.gpsimd.memset(tab_sc[:].bitcast(I32), 0)
         nc.gpsimd.memset(wd_sc_raw[:].bitcast(I32), 0)
+        banks = [psum.tile([P, BANK], F32, name="bank%d" % i) for i in range(8)]
 
-        def load_scale_rows(queue, tile, scales):
+        def load_scale_rows(tile, scales):
             for q in range(4):
-                queue.dma_start(
+                nc.sync.dma_start(
                     out=tile[32 * q : 32 * q + 8, :].bitcast(I32), in_=scales[:, 4 * q : 4 * q + 4, :].bitcast(I32)
                 )
 
+        warm = keep.tile([P, 2], F32, name="warm")
+        nc.vector.memset(warm[:], 0.0)
+        nc.scalar.activation(warm[:, 1:2], warm[:, 0:1], SILU)
         nc.sync.dma_start(src_list[:], offs)
         nc.sync.dma_start(dst_list[:], offs2)
 
-        tab_w = [keep.tile([P, T], I32, name="tab_w%d" % a, align_bytes=64) for a in range(2)]
+        tab_w = [placed("tab_w%d" % a, [P, T], I32, TAB_AT + a * BIG) for a in range(2)]
 
         def load_tab(a, parts):
             words = tab_words[a].rearrange("p t i -> p (t i)").bitcast(I32)
             for q in range(parts):
-                cols = slice(q * T // parts // 64 * 64, (q + 1) * T // parts // 64 * 64)
+                cols = slice(q * T // parts, (q + 1) * T // parts)
                 nc.sync.dma_start(out=tab_w[a][:, cols], in_=words[:, cols])
 
         pieces = [(b, side, a) for b in range(2) for a in range(2) for side in range(2)]
@@ -67,36 +84,47 @@ def tile_list_msg_silu_gateP_kernel(
         def load_piece(n):
             b, side, a = pieces[n]
             w = (ws, wt)[side]
-            raw[n] = ring.tile([P, PACK, PASS], F32, name="w_raw", tag="big%d" % (0, 1, 2, 3, 4, 5, 1, 2)[n], bufs=1, align_bytes=64)
+            raw[n] = placed("w_raw%d" % n, [P, PACK, PASS], F32, n * BIG)
             rows = w[a * PASS : (a + 1) * PASS, b * PASS : (b + 1) * PASS].rearrange("(p i) c -> p i c", i=PACK)
             nc.sync.dma_start(out=raw[n][:], in_=rows)
 
-        sm_sb = keep.tile([P, 2, PACK], F32, name="sm_sb")
-        nc.sync.dma_start(out=sm_sb[:], in_=sm.rearrange("(b p t) -> p b t", p=P, t=PACK))
+        load_tab(0, 4)
         wgo_row = keep.tile([P, J // P], F32, name="wgo_row")
         nc.sync.dma_start(out=wgo_row[:], in_=wgo[0].rearrange("(p e) -> p e", p=P))
         identity = keep.tile([P, P], F32, name="identity")
         make_identity(nc, identity[:])
-        load_tab(0, 3)
-        load_scale_rows(nc.sync, tab_sc, tab_scales)
+        load_scale_rows(tab_sc, tab_scales)
         load_piece(0)
         load_piece(1)
-        load_tab(1, 1)
+        sm_sb = [keep.tile([P, PACK], F32, name="sm_sb%d" % b) for b in range(2)]
+        sm_rows = sm.rearrange("(b p t) -> b p t", p=P, t=PACK)
+        for b in range(2):
+            nc.sync.dma_start(out=sm_sb[b][:], in_=sm_rows[b])
         load_piece(2)
-        load_piece(3)
-        load_piece(4)
-        load_piece(5)
+        load_tab(1, 1)
+        g_rows = {}
+
+        def load_gate_rows(t):
+            g_rows[t] = placed("g_rows%d" % t, [P, T], F32, (3 - t) * BIG)
+            nc.sync.dma_start(out=g_rows[t][:], in_=gT.rearrange("(p t) c -> p t c", t=PACK)[:, t, :])
+
+        for n in range(3, 8):
+            load_piece(n)
         wd_raw = keep.tile([P, 2, N], I32, name="wd_raw", align_bytes=64)
         nc.sync.dma_start(out=wd_raw[:], in_=wd_words.rearrange("a p n i -> p a (n i)").bitcast(I32))
-        load_scale_rows(nc.sync, wd_sc_raw, wd_scales)
+        load_scale_rows(wd_sc_raw, wd_scales)
+        for t in (3, 2, 1):
+            load_gate_rows(t)
+        load_gate_rows(0)
+
         wgo_sb = keep.tile([P, J], F32, name="wgo_sb")
         for half in range(2):
-            spread = psum.tile([P, PACK, P], F32, name="spread", tag="a0", bufs=4)
+            spread = banks[4 + half][:].rearrange("q (e p) -> q e p", e=PACK)
             for e in range(PACK):
                 column = PACK * half + e
                 nc.tensor.transpose(spread[:, e, :], wgo_row[:, column : column + 1].to_broadcast([P, P]), identity[:])
             nc.scalar.copy(
-                wgo_sb[:].rearrange("q (p h e) -> q h p e", h=2, e=PACK)[:, half], spread[:].rearrange("q e p -> q p e")
+                wgo_sb[:].rearrange("q (p h e) -> q h p e", h=2, e=PACK)[:, half], spread.rearrange("q e p -> q p e")
             )
 
         pages = [keep.tile([P, T], F32, name="page%d" % t) for t in range(PACK)]
@@ -107,133 +135,140 @@ def tile_list_msg_silu_gateP_kernel(
         v_scales = {}
 
         def gather_words(side, a):
-            v_words[side, a] = ring.tile([P, J], U32, name="v_words", tag="words%d%d" % (side, a), bufs=1, align_bytes=64)
-            nc.vector.tensor_copy(v_words[side, a][:], tab_w[a][:].bitcast(U32).indirect(lists[side][:]))
+            words = keep.tile([P, J], U32, name="v_words%d%d" % (side, a), align_bytes=64)
+            nc.vector.tensor_copy(words[:], tab_w[a][:].bitcast(U32).indirect(lists[side][:]))
+            v_words[side, a, 0] = words[:, 0:HALF]
+            v_words[side, a, 1] = words[:, HALF:J]
 
-        def gather_scales():
-            for side in range(2):
-                v_scales[side] = keep.tile([P, J], U8, name="v_scales%d" % side, align_bytes=64)
-                nc.vector.tensor_copy(v_scales[side][:], tab_sc[:].indirect(lists[side][:]))
+        def gather_half(side, a, half, words):
+            offsets = lists[side][:, half * HALF // 16 : (half + 1) * HALF // 16]
+            nc.vector.tensor_copy(words[:], tab_w[a][:].bitcast(U32).indirect(offsets))
+            v_words[side, a, half] = words[:]
+
+        def gather_scales(side):
+            v_scales[side] = keep.tile([P, J], U8, name="v_scales%d" % side, align_bytes=64)
+            nc.vector.tensor_copy(v_scales[side][:], tab_sc[:].indirect(lists[side][:]))
 
         w_codes = {}
         w_scales = {}
         w_bf = {}
 
         def cast_piece(n):
-            w_bf[n] = ring.tile([P, PACK * PASS], BF16, name="w_bf", tag=("qin0", "qin1", "words11", "qin3", "qin3", "qin0", "qin1", "qin2")[n], bufs=1, align_bytes=64)
+            w_bf[n] = placed("w_bf%d" % n, [P, PACK * PASS], BF16, QIN_AT + n % QIN_SLOTS * QIN)
             dst = w_bf[n][:].rearrange("p (u e m i) -> p u m i e", u=2, e=2, i=PACK)
             src = raw[n][:].rearrange("p i (m u e) -> p u m i e", u=2, e=2)
             if n < SCALAR_CASTS:
                 nc.scalar.copy(dst, src)
             else:
-                nc.vector.tensor_copy(dst, src)
+                for u in range(2):
+                    nc.vector.tensor_copy(dst[:, u], src[:, u])
 
-        def quant_piece(n):
-            w_codes[n] = keep.tile([P, PASS], U32, name="w_codes%d" % n, align_bytes=64)
+        def quant_piece(n, at=None):
+            if at is None:
+                w_codes[n] = keep.tile([P, PASS], U32, name="w_codes%d" % n, align_bytes=64)
+            else:
+                w_codes[n] = placed("w_codes%d" % n, [P, PASS], U32, at)
             w_scales[n] = keep.tile([P, PASS], U8, name="w_scales%d" % n, align_bytes=64)
-            nc.vector.quantize_mx(out=w_codes[n][:].bitcast(FP8X4), scales=w_scales[n][:], in_=w_bf[n][:])
+            parts = 1 if n < SCALAR_CASTS else 2
+            for u in range(parts):
+                cols = slice(u * PASS // parts, (u + 1) * PASS // parts)
+                nc.vector.quantize_mx(
+                    out=w_codes[n][:, cols].bitcast(FP8X4),
+                    scales=w_scales[n][:, cols],
+                    in_=w_bf[n][:, PACK * cols.start : PACK * cols.stop],
+                )
 
         gather_words(0, 0)
         gather_words(1, 0)
-        gather_scales()
-        for n in range(2):
+        gather_scales(0)
+        gather_scales(1)
+        for n in range(3):
             cast_piece(n)
             quant_piece(n)
         gather_words(0, 1)
-        cast_piece(2)
-        quant_piece(2)
-        gather_words(1, 1)
+        gather_half(1, 1, 0, keep.tile([P, HALF], U32, name="v_words110", align_bytes=64))
         cast_piece(3)
         quant_piece(3)
-        g_rows = {}
+        gather_half(1, 1, 1, placed("v_words111", [P, HALF], U32, QIN_AT + 3 * QIN))
+
         gates = {}
 
-        def load_gate_rows(t, tag):
-            g_rows[t] = ring.tile([P, T], F32, name="g_rows", tag=tag, bufs=1, align_bytes=64)
-            nc.sync.dma_start(out=g_rows[t][:], in_=gT.rearrange("(p t) c -> p t c", t=PACK)[:, t, :])
-
-        def gate(t, tag):
-            gates[t] = ring.tile([P, J], F32, name="gate", tag=tag, bufs=1, align_bytes=64)
+        def gate(t, at=None):
+            if at is None:
+                gates[t] = keep.tile([P, J], F32, name="gate%d" % t, align_bytes=64)
+            else:
+                gates[t] = placed("gate%d" % t, [P, J], F32, at)
             nc.vector.tensor_tensor(gates[t][:], g_rows[t][:].indirect(src_list[:]), wgo_sb[:], MULT)
-
-        load_gate_rows(2, "big0")
-        load_piece(6)
-        load_piece(7)
-        cast_piece(4)
-        cast_piece(5)
-        quant_piece(4)
-        quant_piece(5)
-        load_gate_rows(3, "big4")
-        load_gate_rows(1, "big5")
-        gate(2, "gate2")
-        load_gate_rows(0, "big0")
-        cast_piece(6)
-        cast_piece(7)
-        quant_piece(6)
-        quant_piece(7)
 
         wd_w = keep.tile([P, 2, N], I32, name="wd_w", align_bytes=64)
         wd_sc = keep.tile([P, N], U8, name="wd_sc", align_bytes=64)
-        nc.vector.tensor_copy(
-            wd_w[:].rearrange("p a (u e m) -> p u a m e", u=2, e=2),
-            wd_raw[:].rearrange("p a (m u e) -> p u a m e", u=2, e=2),
-        )
-        nc.vector.tensor_copy(
-            wd_sc[:].rearrange("p (t m) -> p t m", t=PACK), wd_sc_raw[:].rearrange("p (m t) -> p t m", t=PACK)
-        )
+
+        def sort_wd():
+            nc.vector.tensor_copy(
+                wd_w[:].rearrange("p a (u e m) -> p u a m e", u=2, e=2),
+                wd_raw[:].rearrange("p a (m u e) -> p u a m e", u=2, e=2),
+            )
+            nc.vector.tensor_copy(
+                wd_sc[:].rearrange("p (t m) -> p t m", t=PACK), wd_sc_raw[:].rearrange("p (m t) -> p t m", t=PACK)
+            )
 
         h_codes = {}
         h_scales = {}
         h_rows = {}
-        per_bank_bufs = (4, 2)
+        turn = []
 
-        def activate(b, j0, width, t0):
+        def activate(b, j0, width, t0, rows_at):
             cols = slice(j0, j0 + width)
             per_bank = BANK // width
             if t0 == 0:
-                h_rows[b, j0] = ring.tile([P, PACK, width], BF16, name="h_rows", tag="rows%d_%d" % (b, j0), bufs=1, align_bytes=64)
-            bank = psum.tile([P, per_bank, width], F32, name="a_bank", tag="a%d" % b, bufs=per_bank_bufs[b])
+                h_rows[b, j0] = placed("h_rows%d_%d" % (b, j0), [P, PACK, width], BF16, rows_at)
+            act_at = ACT_AT + len(turn) % ACTS * 2048
+            bank = banks[len(turn) % A_BANKS]
+            act = placed("act%d" % len(turn), [P, BANK], F32, act_at)
+            turn.append(0)
             for s in range(4):
                 n = 4 * b + s
                 side, a = pieces[n][1:]
                 for u in range(per_bank):
                     rows = slice((t0 + u) * P, (t0 + u + 1) * P)
                     nc.tensor.matmul_mx(
-                        out=bank[:, u, :],
+                        out=bank[:, u * width : (u + 1) * width],
                         lhsT=w_codes[n][:, rows].bitcast(FP8X4),
                         lhsT_scale=w_scales[n][:, rows],
-                        rhs=v_words[side, a][:, cols].bitcast(FP8X4),
+                        rhs=v_words[side, a, j0 // HALF][:, j0 % HALF : j0 % HALF + width].bitcast(FP8X4),
                         rhs_scale=v_scales[side][4 * a : P, cols],
                         start=(s == 0 and u == 0),
                         stop=(s == 3 and u == per_bank - 1),
                     )
-            act = ring.tile([P, per_bank, width], F32, name="act", tag="act", bufs=2)
             nc.scalar.activation(act[:], bank[:], SILU)
             for u in range(per_bank):
                 t = t0 + u
-                nc.scalar.activation(h_rows[b, j0][:, t, :], act[:, u, :], COPY, scale=sm_sb[:, b, t : t + 1])
+                nc.scalar.activation(
+                    h_rows[b, j0][:, t, :], act[:, u * width : (u + 1) * width], COPY, scale=sm_sb[b][:, t : t + 1]
+                )
 
-        def pack(b, j0, width, tag, codes_tag):
-            h_bf = ring.tile([P, PACK * width], BF16, name="h_bf", tag=tag, bufs=1, align_bytes=64)
+        h_bf = {}
+
+        def pack(b, j0, width, at):
+            h_bf[b, j0] = placed("h_bf%d_%d" % (b, j0), [P, PACK * width], BF16, at)
             nc.scalar.copy(
-                h_bf[:].rearrange("p (c i t) -> p c t i", i=4, t=PACK),
+                h_bf[b, j0][:].rearrange("p (c i t) -> p c t i", i=4, t=PACK),
                 h_rows[b, j0][:].rearrange("p t (c i) -> p c t i", i=4),
             )
-            h_codes[b, j0] = ring.tile([P, width], U32, name="h_codes", tag=codes_tag, bufs=1, align_bytes=64)
+
+        def quant_h(b, j0, width, at):
+            h_codes[b, j0] = placed("h_codes%d_%d" % (b, j0), [P, width], U32, at)
             h_scales[b, j0] = keep.tile([P, width], U8, name="h_scales%d_%d" % (b, j0), align_bytes=64)
-            nc.vector.quantize_mx(out=h_codes[b, j0][:].bitcast(FP8X4), scales=h_scales[b, j0][:], in_=h_bf[:])
+            nc.vector.quantize_mx(out=h_codes[b, j0][:].bitcast(FP8X4), scales=h_scales[b, j0][:], in_=h_bf[b, j0][:])
 
-        y_last = keep.tile([P, J], F32, name="y_last")
-
-        def message(c, u, tag="y", bufs=1):
-            bank = psum.tile([P, 2, CHUNK], F32, name="y_bank", tag=tag, bufs=bufs)
-            for e in range(2):
-                rows = slice((2 * u + e) * P, (2 * u + e + 1) * P)
+        def message(c, slots, bank):
+            for e, t in enumerate(slots):
+                rows = slice(t * P, (t + 1) * P)
                 for b in range(2):
                     j0 = c * CHUNK if b else c * CHUNK // HALF * HALF
                     cols = slice(c * CHUNK - j0, (c + 1) * CHUNK - j0)
                     nc.tensor.matmul_mx(
-                        out=bank[:, e, :],
+                        out=bank[:, e * CHUNK : (e + 1) * CHUNK],
                         lhsT=wd_w[:, b, rows].bitcast(FP8X4),
                         lhsT_scale=wd_sc[4 * b : P, rows],
                         rhs=h_codes[b, j0][:, cols].bitcast(FP8X4),
@@ -241,7 +276,6 @@ def tile_list_msg_silu_gateP_kernel(
                         start=(b == 0),
                         stop=(b == 1),
                     )
-            return bank
 
         def scatter(t, y, j0, width):
             nc.vector.tensor_tensor(
@@ -251,73 +285,94 @@ def tile_list_msg_silu_gateP_kernel(
                 MULT,
             )
 
-        def y_tile(shape, tag):
-            return ring.tile(shape, F32, name="y_" + tag, tag=tag, bufs=1, align_bytes=64)
-
-        def deliver(t, c, bank, tag):
-            y = y_tile([P, CHUNK], tag)
-            nc.scalar.copy(y[:], bank[:, t % 2, :])
-            scatter(t, y[:], c * CHUNK, CHUNK)
-
-        def deliver_low(c, tag, bank_tag="y", bank_bufs=1):
-            bank = message(c, 0, bank_tag, bank_bufs)
-            y = y_tile([P, 2, CHUNK], tag)
-            nc.scalar.copy(y[:], bank[:])
-            for t in range(2):
-                scatter(t, y[:, t, :], c * CHUNK, CHUNK)
-
-        def deliver_high(c, y, bank_tag="y", bank_bufs=1):
-            bank = message(c, 1, bank_tag, bank_bufs)
-            nc.scalar.copy(y, bank[:, 0, :])
-            nc.scalar.copy(y_last[:, c * CHUNK : (c + 1) * CHUNK], bank[:, 1, :])
-
+        low, high = slice(0, CHUNK), slice(CHUNK, BANK)
+        rows_a, rows_b, rows_c, rows_d = ROWS_AT, ROWS_AT + QIN, ROWS_AT + 2 * QIN, ROWS_AT + 2 * QIN + QIN // 2
+        cast_piece(4)
+        cast_piece(5)
+        quant_piece(4, 5 * BIG)
+        quant_piece(5)
+        for n in range(6, 8):
+            cast_piece(n)
+            quant_piece(n)
+        sort_wd()
         for t in range(PACK):
-            activate(0, 0, HALF, t)
-        pack(0, 0, HALF, "qin3", "qin2")
-        gate(3, "gate3")
-        gate(1, "gate1")
+            activate(0, 0, HALF, t, rows_a)
+        pack(0, 0, HALF, 4 * BIG)
+        quant_h(0, 0, HALF, QIN_AT + 2 * QIN)
+        gate(3)
+
+        def two(bank):
+            return bank[:].rearrange("p (e c) -> p e c", e=2)
+
+        rows = [CH_AT + c * QIN for c in range(4)]
+        activate(1, 0, CHUNK, 0, rows[0])
+        activate(1, 0, CHUNK, 2, rows[0])
+        pack(1, 0, CHUNK, QIN_AT + 4 * QIN)
+        gate(2)
+        quant_h(1, 0, CHUNK, BIG + 1024)
+        gate(1)
+        message(0, [0, 1], banks[3])
+        message(0, [2, 3], banks[4])
+        y_low0 = placed("y_low0", [P, BANK], F32, 1024)
+        nc.scalar.copy(y_low0[:], banks[3][:])
+        activate(1, CHUNK, CHUNK, 0, rows[1])
+        activate(1, CHUNK, CHUNK, 2, rows[1])
+        pack(1, CHUNK, CHUNK, QIN_AT + 4 * QIN + QIN // 2)
+        quant_h(1, CHUNK, CHUNK, 2 * BIG)
+        gate(0)
+        scatter(1, y_low0[:, high], 0, CHUNK)
+        scatter(0, y_low0[:, low], 0, CHUNK)
+        y_high0 = placed("y_high0", [P, BANK], F32, 2 * BIG + 1024)
+        nc.scalar.copy(y_high0[:], banks[4][:])
+        scatter(2, y_high0[:, low], 0, CHUNK)
+        scatter(3, y_high0[:, high], 0, CHUNK)
+        message(1, [0, 1], banks[5])
+        message(1, [2, 3], banks[6])
         for t in range(PACK):
-            activate(0, HALF, HALF, t)
-        activate(1, 0, CHUNK, 0)
-        activate(1, 0, CHUNK, 2)
-        pack(1, 0, CHUNK, "gate0", "big5")
-        gate(0, "gate0")
-        bank = message(0, 0)
-        deliver(0, 0, bank, "low0")
-        pack(0, HALF, HALF, "rows1_0", "low0")
-        deliver(1, 0, bank, "big0")
-        activate(1, CHUNK, CHUNK, 0)
-        activate(1, CHUNK, CHUNK, 2)
-        pack(1, CHUNK, CHUNK, "qin0", "big0")
-        y02 = y_tile([P, CHUNK], "rows1_256")
-        deliver_high(0, y02[:])
-        scatter(2, y02[:], 0, CHUNK)
-        deliver_low(1, "low1")
-        activate(1, 2 * CHUNK, CHUNK, 0)
-        activate(1, 2 * CHUNK, CHUNK, 2)
-        pack(1, 2 * CHUNK, CHUNK, "qin1", "low1")
-        y12 = y_tile([P, CHUNK], "rows1_512")
-        deliver_high(1, y12[:])
-        scatter(2, y12[:], CHUNK, CHUNK)
-        activate(1, 3 * CHUNK, CHUNK, 0)
-        activate(1, 3 * CHUNK, CHUNK, 2)
-        bank = message(2, 0)
-        deliver(0, 2, bank, "low2")
-        pack(1, 3 * CHUNK, CHUNK, "qin3", "low2")
-        deliver(1, 2, bank, "rows1_768")
-        y23 = y_tile([P, HALF], "high23")
-        deliver_low(3, "low3", "a0", 4)
-        deliver_high(2, y23[:, 0:CHUNK])
-        deliver_high(3, y23[:, CHUNK:HALF], "a0", 4)
-        scatter(2, y23[:], HALF, HALF)
-        scatter(PACK - 1, y_last[:], 0, J)
+            activate(0, HALF, HALF, t, rows_b)
+        pack(0, HALF, HALF, QIN_AT)
+        quant_h(0, HALF, HALF, 5120)
+        y_01 = placed("y_01", [P, CHUNK], F32, rows_b)
+        nc.scalar.copy(y_01[:], banks[5][:, low])
+        scatter(0, y_01[:], CHUNK, CHUNK)
+
+        activate(1, 2 * CHUNK, CHUNK, 0, rows[2])
+        activate(1, 2 * CHUNK, CHUNK, 2, rows[2])
+        pack(1, 2 * CHUNK, CHUNK, QIN_AT + QIN)
+        quant_h(1, 2 * CHUNK, CHUNK, 7168)
+        y_11 = placed("y_11", [P, CHUNK], F32, rows[2] + 1024)
+        nc.scalar.copy(y_11[:], banks[5][:, high])
+        scatter(1, y_11[:], CHUNK, CHUNK)
+        y_late = placed("y_late", [P, 2, 3 * CHUNK], F32, rows[2] - 5120)
+        nc.scalar.copy(y_late[:, :, 0:CHUNK], two(banks[6]))
+        scatter(2, y_late[:, 0, 0:CHUNK], CHUNK, CHUNK)
+
+        activate(1, 3 * CHUNK, CHUNK, 0, rows[3])
+        activate(1, 3 * CHUNK, CHUNK, 2, rows[3])
+        pack(1, 3 * CHUNK, CHUNK, QIN_AT + QIN + QIN // 2)
+        quant_h(1, 3 * CHUNK, CHUNK, BIG)
+        message(2, [0, 1], banks[7])
+        message(3, [0, 1], banks[3])
+        y_02 = placed("y_02", [P, CHUNK], F32, rows[3])
+        y_03 = placed("y_03", [P, CHUNK], F32, rows_a)
+        y_123 = placed("y_123", [P, HALF], F32, rows[3] + 1024)
+        nc.scalar.copy(y_02[:], banks[7][:, low])
+        scatter(0, y_02[:], 2 * CHUNK, CHUNK)
+        nc.scalar.copy(y_123[:, low], banks[7][:, high])
+        nc.scalar.copy(y_03[:], banks[3][:, low])
+        scatter(0, y_03[:], 3 * CHUNK, CHUNK)
+        nc.scalar.copy(y_123[:, high], banks[3][:, high])
+        scatter(1, y_123[:], HALF, HALF)
+        message(2, [2, 3], banks[7])
+        message(3, [2, 3], banks[4])
+        nc.scalar.copy(y_late[:, :, CHUNK : 2 * CHUNK], two(banks[7]))
+        nc.scalar.copy(y_late[:, :, 2 * CHUNK : 3 * CHUNK], two(banks[4]))
+        scatter(2, y_late[:, 0, CHUNK : 3 * CHUNK], HALF, HALF)
+        scatter(PACK - 1, y_late[:, 1, :], CHUNK, 3 * CHUNK)
 
         out_rows = out_0.rearrange("(p t) c -> p t c", t=PACK)
         quarters = T // QUARTER
-        pairs = [
-            ring.tile([P, 2, QUARTER, 2], BF16, name="pairs%d" % q, tag="big%d" % (q + 1), bufs=1, align_bytes=64)
-            for q in range(quarters)
-        ]
+        pairs = [placed("pairs%d" % q, [P, 2, QUARTER, 2], BF16, 6 * BIG + q * QIN) for q in range(quarters)]
         for t in range(PACK):
             nc.sync.dma_start(out=out_rows[:, t, :], in_=pages[t][:])
             for q in range(quarters):
@@ -327,7 +382,7 @@ def tile_list_msg_silu_gateP_kernel(
         o_bf = {}
 
         def weave(q):
-            o_bf[q] = ring.tile([P, PACK * QUARTER], BF16, name="o_bf", tag="qin%d" % (0, 1, 3, 2)[q], bufs=1, align_bytes=64)
+            o_bf[q] = placed("o_bf%d" % q, [P, PACK * QUARTER], BF16, TAB_AT + q * QIN)
             dst = o_bf[q][:].bitcast(F32).rearrange("p (c k u) -> p c u k", k=2, u=2)
             src = pairs[q][:].rearrange("p u c e -> p (u c e)").bitcast(F32).rearrange("p (u c k) -> p c u k", u=2, k=2)
             if q + 1 < quarters:

@@ -34,7 +34,8 @@ ROWS_AT = QIN_AT + QIN_SLOTS * QIN
 ACTS = 2
 A_BANKS = 3
 ACT_AT = ROWS_AT + 2 * QIN
-CH_AT = ACT_AT + ACTS * 2048
+WD_AT = ACT_AT + ACTS * 2048
+CH_AT = WD_AT + QIN
 
 
 def tile_list_msg_silu_gateP_kernel(
@@ -98,8 +99,7 @@ def tile_list_msg_silu_gateP_kernel(
         load_piece(1)
         sm_sb = [keep.tile([P, PACK], F32, name="sm_sb%d" % b) for b in range(2)]
         sm_rows = sm.rearrange("(b p t) -> b p t", p=P, t=PACK)
-        for b in range(2):
-            nc.sync.dma_start(out=sm_sb[b][:], in_=sm_rows[b])
+        nc.sync.dma_start(out=sm_sb[0][:], in_=sm_rows[0])
         load_piece(2)
         load_tab(1, 1)
         g_rows = {}
@@ -110,12 +110,14 @@ def tile_list_msg_silu_gateP_kernel(
 
         for n in range(3, 8):
             load_piece(n)
-        wd_raw = keep.tile([P, 2, N], I32, name="wd_raw", align_bytes=64)
+        load_gate_rows(3)
+        wd_raw = placed("wd_raw", [P, 2, N], I32, WD_AT)
         nc.sync.dma_start(out=wd_raw[:], in_=wd_words.rearrange("a p n i -> p a (n i)").bitcast(I32))
         load_scale_rows(wd_sc_raw, wd_scales)
-        for t in (3, 2, 1):
+        load_gate_rows(2)
+        nc.sync.dma_start(out=sm_sb[1][:], in_=sm_rows[1])
+        for t in (1, 0):
             load_gate_rows(t)
-        load_gate_rows(0)
 
         wgo_sb = keep.tile([P, J], F32, name="wgo_sb")
         for half in range(2):
@@ -294,112 +296,136 @@ def tile_list_msg_silu_gateP_kernel(
         for n in range(6, 8):
             cast_piece(n)
             quant_piece(n)
+        gate(3)
         sort_wd()
         for t in range(PACK):
             activate(0, 0, HALF, t, rows_a)
         pack(0, 0, HALF, 4 * BIG)
-        quant_h(0, 0, HALF, QIN_AT + 2 * QIN)
-        gate(3)
+        quant_h(0, 0, HALF, WD_AT)
 
         def two(bank):
             return bank[:].rearrange("p (e c) -> p e c", e=2)
 
         rows = [CH_AT + c * QIN for c in range(4)]
+        gate(2)
+        gate(1)
+        for t in range(2):
+            activate(0, HALF, HALF, t, rows_b)
         activate(1, 0, CHUNK, 0, rows[0])
         activate(1, 0, CHUNK, 2, rows[0])
         pack(1, 0, CHUNK, QIN_AT + 4 * QIN)
-        gate(2)
-        quant_h(1, 0, CHUNK, BIG + 1024)
-        gate(1)
-        message(0, [0, 1], banks[3])
-        message(0, [2, 3], banks[4])
-        y_low0 = placed("y_low0", [P, BANK], F32, 1024)
-        nc.scalar.copy(y_low0[:], banks[3][:])
+        quant_h(1, 0, CHUNK, 2 * BIG)
+        gate(0)
+        message(0, [0], banks[3])
+        message(0, [1], banks[4])
+        message(0, [2, 3], banks[5])
         activate(1, CHUNK, CHUNK, 0, rows[1])
         activate(1, CHUNK, CHUNK, 2, rows[1])
         pack(1, CHUNK, CHUNK, QIN_AT + 4 * QIN + QIN // 2)
-        quant_h(1, CHUNK, CHUNK, 2 * BIG)
-        gate(0)
-        scatter(1, y_low0[:, high], 0, CHUNK)
-        scatter(0, y_low0[:, low], 0, CHUNK)
-        y_high0 = placed("y_high0", [P, BANK], F32, 2 * BIG + 1024)
-        nc.scalar.copy(y_high0[:], banks[4][:])
+        quant_h(1, CHUNK, CHUNK, 3 * BIG)
+        y_00 = placed("y_00", [P, CHUNK], F32, 0)
+        nc.scalar.copy(y_00[:], banks[3][:, low])
+        scatter(0, y_00[:], 0, CHUNK)
+        y_10 = placed("y_10", [P, CHUNK], F32, 3 * BIG + 1024)
+        nc.scalar.copy(y_10[:], banks[4][:, low])
+        scatter(1, y_10[:], 0, CHUNK)
+        y_high0 = placed("y_high0", [P, BANK], F32, 3 * BIG + 2048)
+        nc.scalar.copy(y_high0[:], banks[5][:])
         scatter(2, y_high0[:, low], 0, CHUNK)
         scatter(3, y_high0[:, high], 0, CHUNK)
-        message(1, [0, 1], banks[5])
-        message(1, [2, 3], banks[6])
-        for t in range(PACK):
+        message(1, [0, 1], banks[6])
+        message(1, [2, 3], banks[7])
+        for t in range(2, PACK):
             activate(0, HALF, HALF, t, rows_b)
         pack(0, HALF, HALF, QIN_AT)
         quant_h(0, HALF, HALF, 5120)
-        y_01 = placed("y_01", [P, CHUNK], F32, rows_b)
-        nc.scalar.copy(y_01[:], banks[5][:, low])
-        scatter(0, y_01[:], CHUNK, CHUNK)
+        y_low1 = placed("y_low1", [P, BANK], F32, rows_b)
+        nc.scalar.copy(y_low1[:], banks[6][:])
+        scatter(0, y_low1[:, low], CHUNK, CHUNK)
+        scatter(1, y_low1[:, high], CHUNK, CHUNK)
 
         activate(1, 2 * CHUNK, CHUNK, 0, rows[2])
         activate(1, 2 * CHUNK, CHUNK, 2, rows[2])
         pack(1, 2 * CHUNK, CHUNK, QIN_AT + QIN)
         quant_h(1, 2 * CHUNK, CHUNK, 7168)
-        y_11 = placed("y_11", [P, CHUNK], F32, rows[2] + 1024)
-        nc.scalar.copy(y_11[:], banks[5][:, high])
-        scatter(1, y_11[:], CHUNK, CHUNK)
         y_late = placed("y_late", [P, 2, 3 * CHUNK], F32, rows[2] - 5120)
-        nc.scalar.copy(y_late[:, :, 0:CHUNK], two(banks[6]))
+        nc.scalar.copy(y_late[:, :, 0:CHUNK], two(banks[7]))
         scatter(2, y_late[:, 0, 0:CHUNK], CHUNK, CHUNK)
 
+        message(2, [0], banks[3])
+        message(2, [1], banks[4])
         activate(1, 3 * CHUNK, CHUNK, 0, rows[3])
         activate(1, 3 * CHUNK, CHUNK, 2, rows[3])
+        y_02 = placed("y_02", [P, CHUNK], F32, ACT_AT + (len(turn) - 1) % ACTS * 2048)
+        nc.scalar.copy(y_02[:], banks[3][:, low])
+        scatter(0, y_02[:], 2 * CHUNK, CHUNK)
         pack(1, 3 * CHUNK, CHUNK, QIN_AT + QIN + QIN // 2)
         quant_h(1, 3 * CHUNK, CHUNK, BIG)
-        message(2, [0, 1], banks[7])
-        message(3, [0, 1], banks[3])
-        y_02 = placed("y_02", [P, CHUNK], F32, rows[3])
+        y_12 = placed("y_12", [P, CHUNK], F32, rows[3])
+        nc.scalar.copy(y_12[:], banks[4][:, low])
+        scatter(1, y_12[:], 2 * CHUNK, CHUNK)
+        message(3, [0], banks[5])
+        message(3, [1], banks[6])
         y_03 = placed("y_03", [P, CHUNK], F32, rows_a)
-        y_123 = placed("y_123", [P, HALF], F32, rows[3] + 1024)
-        nc.scalar.copy(y_02[:], banks[7][:, low])
-        scatter(0, y_02[:], 2 * CHUNK, CHUNK)
-        nc.scalar.copy(y_123[:, low], banks[7][:, high])
-        nc.scalar.copy(y_03[:], banks[3][:, low])
+        nc.scalar.copy(y_03[:], banks[5][:, low])
         scatter(0, y_03[:], 3 * CHUNK, CHUNK)
-        nc.scalar.copy(y_123[:, high], banks[3][:, high])
-        scatter(1, y_123[:], HALF, HALF)
-        message(2, [2, 3], banks[7])
-        message(3, [2, 3], banks[4])
-        nc.scalar.copy(y_late[:, :, CHUNK : 2 * CHUNK], two(banks[7]))
-        nc.scalar.copy(y_late[:, :, 2 * CHUNK : 3 * CHUNK], two(banks[4]))
+        y_13 = placed("y_13", [P, CHUNK], F32, rows_a + 1024)
+        nc.scalar.copy(y_13[:], banks[6][:, low])
+        scatter(1, y_13[:], 3 * CHUNK, CHUNK)
+        message(2, [2, 3], banks[4])
+        message(3, [2, 3], banks[3])
+        nc.scalar.copy(y_late[:, :, CHUNK : 2 * CHUNK], two(banks[4]))
+        nc.scalar.copy(y_late[:, :, 2 * CHUNK : 3 * CHUNK], two(banks[3]))
         scatter(2, y_late[:, 0, CHUNK : 3 * CHUNK], HALF, HALF)
         scatter(PACK - 1, y_late[:, 1, :], CHUNK, 3 * CHUNK)
 
         out_rows = out_0.rearrange("(p t) c -> p t c", t=PACK)
         quarters = T // QUARTER
         pairs = [placed("pairs%d" % q, [P, 2, QUARTER, 2], BF16, 6 * BIG + q * QIN) for q in range(quarters)]
+
+        def round_page(t, q, c0, c1):
+            nc.scalar.copy(pairs[q][:, t // 2, c0:c1, t % 2], pages[t][:, q * QUARTER + c0 : q * QUARTER + c1])
+
         for t in range(PACK):
             nc.sync.dma_start(out=out_rows[:, t, :], in_=pages[t][:])
             for q in range(quarters):
-                nc.scalar.copy(pairs[q][:, t // 2, :, t % 2], pages[t][:, q * QUARTER : (q + 1) * QUARTER])
-        o_scales = keep.tile([P, QUARTER], U8, name="o_scales", align_bytes=64)
+                if t == PACK - 1 and q == 0:
+                    round_page(t, q, 0, CHUNK)
+                    round_page(t, q, CHUNK, QUARTER)
+                else:
+                    round_page(t, q, 0, QUARTER)
+        o_scales = keep.tile([P, 2 * QUARTER], U8, name="o_scales", align_bytes=64)
         out_words = out_1[0].rearrange("p c i -> p (c i)").bitcast(I32)
-        o_bf = {}
+        o_bf = [placed("o_bf%d" % q, [P, PACK * QUARTER], BF16, TAB_AT + q * QIN) for q in range(quarters)]
+        o_codes = [keep.tile([P, QUARTER], U32, name="o_codes%d" % q, align_bytes=64) for q in range(quarters)]
 
-        def weave(q):
-            o_bf[q] = placed("o_bf%d" % q, [P, PACK * QUARTER], BF16, TAB_AT + q * QIN)
+        def weave(copy, q, c0, c1):
             dst = o_bf[q][:].bitcast(F32).rearrange("p (c k u) -> p c u k", k=2, u=2)
             src = pairs[q][:].rearrange("p u c e -> p (u c e)").bitcast(F32).rearrange("p (u c k) -> p c u k", u=2, k=2)
-            if q + 1 < quarters:
-                nc.vector.tensor_copy(dst, src)
-            else:
-                nc.scalar.copy(dst, src)
+            copy(dst[:, c0 // 2 : c1 // 2], src[:, c0 // 2 : c1 // 2])
 
-        weave(0)
-        for q in range(quarters):
-            if q + 1 < quarters:
-                weave(q + 1)
-            cols = slice(q * QUARTER, (q + 1) * QUARTER)
-            o_codes = keep.tile([P, QUARTER], U32, name="o_codes%d" % q, align_bytes=64)
-            nc.vector.quantize_mx(out=o_codes[:].bitcast(FP8X4), scales=o_scales[4 * q : P, :], in_=o_bf[q][:])
-            nc.sync.dma_start(out=out_words[:, cols], in_=o_codes[:].bitcast(I32))
+        def quant_out(q, c0, c1):
+            at = q % 2 * QUARTER
+            nc.vector.quantize_mx(
+                out=o_codes[q][:, c0:c1].bitcast(FP8X4),
+                scales=o_scales[4 * (q // 2) : P, at + c0 : at + c1],
+                in_=o_bf[q][:, PACK * c0 : PACK * c1],
+            )
+            nc.sync.dma_start(out=out_words[:, q * QUARTER + c0 : q * QUARTER + c1], in_=o_codes[q][:, c0:c1].bitcast(I32))
+
+        weave(nc.vector.tensor_copy, 0, 0, CHUNK)
+        weave(nc.vector.tensor_copy, 0, CHUNK, QUARTER)
+        quant_out(0, 0, QUARTER)
+        weave(nc.vector.tensor_copy, 1, 0, QUARTER)
+        weave(nc.vector.tensor_copy, 2, 0, QUARTER)
+        quant_out(1, 0, QUARTER)
+        weave(nc.scalar.copy, 3, 0, CHUNK)
+        weave(nc.scalar.copy, 3, CHUNK, QUARTER)
+        quant_out(2, 0, QUARTER)
+        quant_out(3, 0, CHUNK)
+        quant_out(3, CHUNK, QUARTER)
         for q in range(4):
             nc.scalar.dma_start(
-                out=out_2[0, 4 * q : 4 * q + 4, :].bitcast(I32).rearrange("r (g c) -> g r c", g=quarters),
-                in_=o_scales[32 * q : 32 * q + 16, :].bitcast(I32),
+                out=out_2[0, 4 * q : 4 * q + 4, :].bitcast(I32).rearrange("r (g c) -> g r c", g=2),
+                in_=o_scales[32 * q : 32 * q + 8, :].bitcast(I32),
             )

@@ -35,7 +35,8 @@ ACTS = 2
 A_BANKS = 3
 ACT_AT = ROWS_AT + 2 * QIN
 WD_AT = ACT_AT + ACTS * 2048
-CH_AT = WD_AT + QIN
+SC_AT = WD_AT + QIN + 1024
+CH_AT = SC_AT + 3072
 
 
 def tile_list_msg_silu_gateP_kernel(
@@ -53,15 +54,15 @@ def tile_list_msg_silu_gateP_kernel(
         src_list = keep.tile([P, J // 16], U16, name="src_list")
         dst_list = keep.tile([P, J // 16], U16, name="dst_list")
         lists = (src_list, dst_list)
-        tab_sc = keep.tile([P, T], U8, name="tab_sc", align_bytes=64)
+        tab_sc = placed("tab_sc", [P, T], U8, SC_AT)
         wd_sc_raw = keep.tile([P, N], U8, name="wd_sc_raw", align_bytes=64)
         nc.gpsimd.memset(tab_sc[:].bitcast(I32), 0)
         nc.gpsimd.memset(wd_sc_raw[:].bitcast(I32), 0)
         banks = [psum.tile([P, BANK], F32, name="bank%d" % i) for i in range(8)]
 
-        def load_scale_rows(tile, scales):
-            for q in range(4):
-                nc.sync.dma_start(
+        def load_scale_rows(queue, tile, scales):
+            for q in (0, 2, 1, 3):
+                queue.dma_start(
                     out=tile[32 * q : 32 * q + 8, :].bitcast(I32), in_=scales[:, 4 * q : 4 * q + 4, :].bitcast(I32)
                 )
 
@@ -92,32 +93,33 @@ def tile_list_msg_silu_gateP_kernel(
         load_tab(0, 4)
         wgo_row = keep.tile([P, J // P], F32, name="wgo_row")
         nc.sync.dma_start(out=wgo_row[:], in_=wgo[0].rearrange("(p e) -> p e", p=P))
-        identity = keep.tile([P, P], F32, name="identity")
-        make_identity(nc, identity[:])
-        load_scale_rows(tab_sc, tab_scales)
-        load_piece(0)
-        load_piece(1)
         sm_sb = [keep.tile([P, PACK], F32, name="sm_sb%d" % b) for b in range(2)]
         sm_rows = sm.rearrange("(b p t) -> b p t", p=P, t=PACK)
-        nc.sync.dma_start(out=sm_sb[0][:], in_=sm_rows[0])
+        identity = keep.tile([P, P], F32, name="identity")
+        make_identity(nc, identity[:])
+        load_scale_rows(nc.sync, tab_sc, tab_scales)
+        load_piece(0)
+        load_piece(1)
         load_piece(2)
         load_tab(1, 1)
         g_rows = {}
 
         def load_gate_rows(t):
-            g_rows[t] = placed("g_rows%d" % t, [P, T], F32, (3 - t) * BIG)
+            g_rows[t] = placed("g_rows%d" % t, [P, T], F32, (4, 2, 1, 0)[t] * BIG)
             nc.sync.dma_start(out=g_rows[t][:], in_=gT.rearrange("(p t) c -> p t c", t=PACK)[:, t, :])
 
-        for n in range(3, 8):
+        load_piece(3)
+        load_piece(4)
+        nc.sync.dma_start(out=sm_sb[0][:], in_=sm_rows[0])
+        for n in range(5, 8):
             load_piece(n)
-        load_gate_rows(3)
+        for t in (3, 2, 1):
+            load_gate_rows(t)
+        nc.sync.dma_start(out=sm_sb[1][:], in_=sm_rows[1])
         wd_raw = placed("wd_raw", [P, 2, N], I32, WD_AT)
         nc.sync.dma_start(out=wd_raw[:], in_=wd_words.rearrange("a p n i -> p a (n i)").bitcast(I32))
-        load_scale_rows(wd_sc_raw, wd_scales)
-        load_gate_rows(2)
-        nc.sync.dma_start(out=sm_sb[1][:], in_=sm_rows[1])
-        for t in (1, 0):
-            load_gate_rows(t)
+        load_scale_rows(nc.sync, wd_sc_raw, wd_scales)
+        load_gate_rows(0)
 
         wgo_sb = keep.tile([P, J], F32, name="wgo_sb")
         for half in range(2):
@@ -186,12 +188,12 @@ def tile_list_msg_silu_gateP_kernel(
         gather_scales(1)
         for n in range(3):
             cast_piece(n)
-            quant_piece(n)
+            quant_piece(n, None)
         gather_words(0, 1)
         gather_half(1, 1, 0, keep.tile([P, HALF], U32, name="v_words110", align_bytes=64))
         cast_piece(3)
         quant_piece(3)
-        gather_half(1, 1, 1, placed("v_words111", [P, HALF], U32, QIN_AT + 3 * QIN))
+        gather_half(1, 1, 1, placed("v_words111", [P, HALF], U32, 3 * BIG))
 
         gates = {}
 
@@ -219,13 +221,14 @@ def tile_list_msg_silu_gateP_kernel(
         h_rows = {}
         turn = []
 
-        def activate(b, j0, width, t0, rows_at):
+        def activate(b, j0, width, t0, rows_at, act_at=None):
             cols = slice(j0, j0 + width)
             per_bank = BANK // width
             if t0 == 0:
                 h_rows[b, j0] = placed("h_rows%d_%d" % (b, j0), [P, PACK, width], BF16, rows_at)
-            act_at = ACT_AT + len(turn) % ACTS * 2048
-            bank = banks[len(turn) % A_BANKS]
+            if act_at is None:
+                act_at = ACT_AT + len(turn) % ACTS * 2048
+            bank = banks[(0, 1, 2, 0, 1, 2, 0, 3, 1, 6, 7, 3, 1, 2, 3, 0)[len(turn)]]
             act = placed("act%d" % len(turn), [P, BANK], F32, act_at)
             turn.append(0)
             for s in range(4):
@@ -297,46 +300,45 @@ def tile_list_msg_silu_gateP_kernel(
             cast_piece(n)
             quant_piece(n)
         gate(3)
-        sort_wd()
         for t in range(PACK):
             activate(0, 0, HALF, t, rows_a)
-        pack(0, 0, HALF, 4 * BIG)
-        quant_h(0, 0, HALF, WD_AT)
+        pack(0, 0, HALF, QIN_AT + 3 * QIN)
+        quant_h(0, 0, HALF, 3072)
 
         def two(bank):
             return bank[:].rearrange("p (e c) -> p e c", e=2)
 
-        rows = [CH_AT + c * QIN for c in range(4)]
+        rows = [CH_AT, CH_AT + 2048, CH_AT + QIN, CH_AT + QIN + 7168]
         gate(2)
         gate(1)
-        for t in range(2):
+        sort_wd()
+        for t in range(3):
             activate(0, HALF, HALF, t, rows_b)
         activate(1, 0, CHUNK, 0, rows[0])
         activate(1, 0, CHUNK, 2, rows[0])
         pack(1, 0, CHUNK, QIN_AT + 4 * QIN)
-        quant_h(1, 0, CHUNK, 2 * BIG)
+        quant_h(1, 0, CHUNK, WD_AT)
         gate(0)
-        message(0, [0], banks[3])
-        message(0, [1], banks[4])
+        message(0, [0], banks[2])
+        message(0, [1], banks[0])
         message(0, [2, 3], banks[5])
         activate(1, CHUNK, CHUNK, 0, rows[1])
         activate(1, CHUNK, CHUNK, 2, rows[1])
         pack(1, CHUNK, CHUNK, QIN_AT + 4 * QIN + QIN // 2)
-        quant_h(1, CHUNK, CHUNK, 3 * BIG)
-        y_00 = placed("y_00", [P, CHUNK], F32, 0)
-        nc.scalar.copy(y_00[:], banks[3][:, low])
+        y_00 = placed("y_00", [P, CHUNK], F32, rows[1])
+        nc.scalar.copy(y_00[:], banks[2][:, low])
         scatter(0, y_00[:], 0, CHUNK)
-        y_10 = placed("y_10", [P, CHUNK], F32, 3 * BIG + 1024)
-        nc.scalar.copy(y_10[:], banks[4][:, low])
+        quant_h(1, CHUNK, CHUNK, 4 * BIG)
+        y_10 = placed("y_10", [P, CHUNK], F32, 4 * BIG + 1024)
+        nc.scalar.copy(y_10[:], banks[0][:, low])
         scatter(1, y_10[:], 0, CHUNK)
-        y_high0 = placed("y_high0", [P, BANK], F32, 3 * BIG + 2048)
+        y_high0 = placed("y_high0", [P, BANK], F32, 4 * BIG + 2048)
         nc.scalar.copy(y_high0[:], banks[5][:])
         scatter(2, y_high0[:, low], 0, CHUNK)
         scatter(3, y_high0[:, high], 0, CHUNK)
         message(1, [0, 1], banks[6])
         message(1, [2, 3], banks[7])
-        for t in range(2, PACK):
-            activate(0, HALF, HALF, t, rows_b)
+        activate(0, HALF, HALF, 3, rows_b, 4 * BIG + QIN)
         pack(0, HALF, HALF, QIN_AT)
         quant_h(0, HALF, HALF, 5120)
         y_low1 = placed("y_low1", [P, BANK], F32, rows_b)
@@ -348,16 +350,16 @@ def tile_list_msg_silu_gateP_kernel(
         activate(1, 2 * CHUNK, CHUNK, 2, rows[2])
         pack(1, 2 * CHUNK, CHUNK, QIN_AT + QIN)
         quant_h(1, 2 * CHUNK, CHUNK, 7168)
-        y_late = placed("y_late", [P, 2, 3 * CHUNK], F32, rows[2] - 5120)
+        y_late = placed("y_late", [P, 2, 3 * CHUNK], F32, rows[2] + 1024)
         nc.scalar.copy(y_late[:, :, 0:CHUNK], two(banks[7]))
         scatter(2, y_late[:, 0, 0:CHUNK], CHUNK, CHUNK)
 
-        message(2, [0], banks[3])
+        message(2, [0], banks[2])
         message(2, [1], banks[4])
         activate(1, 3 * CHUNK, CHUNK, 0, rows[3])
         activate(1, 3 * CHUNK, CHUNK, 2, rows[3])
         y_02 = placed("y_02", [P, CHUNK], F32, ACT_AT + (len(turn) - 1) % ACTS * 2048)
-        nc.scalar.copy(y_02[:], banks[3][:, low])
+        nc.scalar.copy(y_02[:], banks[2][:, low])
         scatter(0, y_02[:], 2 * CHUNK, CHUNK)
         pack(1, 3 * CHUNK, CHUNK, QIN_AT + QIN + QIN // 2)
         quant_h(1, 3 * CHUNK, CHUNK, BIG)
@@ -373,9 +375,9 @@ def tile_list_msg_silu_gateP_kernel(
         nc.scalar.copy(y_13[:], banks[6][:, low])
         scatter(1, y_13[:], 3 * CHUNK, CHUNK)
         message(2, [2, 3], banks[4])
-        message(3, [2, 3], banks[3])
+        message(3, [2, 3], banks[2])
         nc.scalar.copy(y_late[:, :, CHUNK : 2 * CHUNK], two(banks[4]))
-        nc.scalar.copy(y_late[:, :, 2 * CHUNK : 3 * CHUNK], two(banks[3]))
+        nc.scalar.copy(y_late[:, :, 2 * CHUNK : 3 * CHUNK], two(banks[2]))
         scatter(2, y_late[:, 0, CHUNK : 3 * CHUNK], HALF, HALF)
         scatter(PACK - 1, y_late[:, 1, :], CHUNK, 3 * CHUNK)
 
@@ -383,17 +385,13 @@ def tile_list_msg_silu_gateP_kernel(
         quarters = T // QUARTER
         pairs = [placed("pairs%d" % q, [P, 2, QUARTER, 2], BF16, 6 * BIG + q * QIN) for q in range(quarters)]
 
-        def round_page(t, q, c0, c1):
-            nc.scalar.copy(pairs[q][:, t // 2, c0:c1, t % 2], pages[t][:, q * QUARTER + c0 : q * QUARTER + c1])
+        def round_page(copy, t, q):
+            copy(pairs[q][:, t // 2, :, t % 2], pages[t][:, q * QUARTER : (q + 1) * QUARTER])
 
         for t in range(PACK):
             nc.sync.dma_start(out=out_rows[:, t, :], in_=pages[t][:])
             for q in range(quarters):
-                if t == PACK - 1 and q == 0:
-                    round_page(t, q, 0, CHUNK)
-                    round_page(t, q, CHUNK, QUARTER)
-                else:
-                    round_page(t, q, 0, QUARTER)
+                round_page(nc.vector.tensor_copy if t >= 2 and q == 0 else nc.scalar.copy, t, q)
         o_scales = keep.tile([P, 2 * QUARTER], U8, name="o_scales", align_bytes=64)
         out_words = out_1[0].rearrange("p c i -> p (c i)").bitcast(I32)
         o_bf = [placed("o_bf%d" % q, [P, PACK * QUARTER], BF16, TAB_AT + q * QIN) for q in range(quarters)]
@@ -413,11 +411,11 @@ def tile_list_msg_silu_gateP_kernel(
             )
             nc.sync.dma_start(out=out_words[:, q * QUARTER + c0 : q * QUARTER + c1], in_=o_codes[q][:, c0:c1].bitcast(I32))
 
-        weave(nc.vector.tensor_copy, 0, 0, CHUNK)
-        weave(nc.vector.tensor_copy, 0, CHUNK, QUARTER)
-        quant_out(0, 0, QUARTER)
+        weave(nc.vector.tensor_copy, 0, 0, QUARTER)
         weave(nc.vector.tensor_copy, 1, 0, QUARTER)
-        weave(nc.vector.tensor_copy, 2, 0, QUARTER)
+        quant_out(0, 0, QUARTER)
+        weave(nc.vector.tensor_copy, 2, 0, CHUNK)
+        weave(nc.scalar.copy, 2, CHUNK, QUARTER)
         quant_out(1, 0, QUARTER)
         weave(nc.scalar.copy, 3, 0, CHUNK)
         weave(nc.scalar.copy, 3, CHUNK, QUARTER)
@@ -425,7 +423,7 @@ def tile_list_msg_silu_gateP_kernel(
         quant_out(3, 0, CHUNK)
         quant_out(3, CHUNK, QUARTER)
         for q in range(4):
-            nc.scalar.dma_start(
+            (nc.scalar, nc.sync)[q % 2].dma_start(
                 out=out_2[0, 4 * q : 4 * q + 4, :].bitcast(I32).rearrange("r (g c) -> g r c", g=2),
                 in_=o_scales[32 * q : 32 * q + 8, :].bitcast(I32),
             )

@@ -189,20 +189,21 @@ def tile_list_msg_silu_gateP_kernel(
         for n in range(3):
             cast_piece(n)
             quant_piece(n, None)
-        gather_words(0, 1)
-        gather_half(1, 1, 0, keep.tile([P, HALF], U32, name="v_words110", align_bytes=64))
+        for side in range(2):
+            gather_half(side, 1, 0, keep.tile([P, HALF], U32, name="v_words%d10" % side, align_bytes=64))
         cast_piece(3)
         quant_piece(3)
-        gather_half(1, 1, 1, placed("v_words111", [P, HALF], U32, 3 * BIG))
+        for side in range(2):
+            gather_half(side, 1, 1, placed("v_words%d11" % side, [P, HALF], U32, 3 * BIG + side * 2048))
 
         gates = {}
 
-        def gate(t, at=None):
-            if at is None:
-                gates[t] = keep.tile([P, J], F32, name="gate%d" % t, align_bytes=64)
-            else:
-                gates[t] = placed("gate%d" % t, [P, J], F32, at)
-            nc.vector.tensor_tensor(gates[t][:], g_rows[t][:].indirect(src_list[:]), wgo_sb[:], MULT)
+        def gate(t, parts=1):
+            gates[t] = keep.tile([P, J], F32, name="gate%d" % t, align_bytes=64)
+            for e in range(parts):
+                cols = slice(e * J // parts, (e + 1) * J // parts)
+                offsets = src_list[:, cols.start // 16 : cols.stop // 16]
+                nc.vector.tensor_tensor(gates[t][:, cols], g_rows[t][:].indirect(offsets), wgo_sb[:, cols], MULT)
 
         wd_w = keep.tile([P, 2, N], I32, name="wd_w", align_bytes=64)
         wd_sc = keep.tile([P, N], U8, name="wd_sc", align_bytes=64)
@@ -294,16 +295,16 @@ def tile_list_msg_silu_gateP_kernel(
         rows_a, rows_b, rows_c, rows_d = ROWS_AT, ROWS_AT + QIN, ROWS_AT + 2 * QIN, ROWS_AT + 2 * QIN + QIN // 2
         cast_piece(4)
         cast_piece(5)
-        quant_piece(4, 5 * BIG)
         quant_piece(5)
+        quant_piece(4, 5 * BIG)
         for n in range(6, 8):
             cast_piece(n)
             quant_piece(n)
-        gate(3)
         for t in range(PACK):
             activate(0, 0, HALF, t, rows_a)
         pack(0, 0, HALF, QIN_AT + 3 * QIN)
-        quant_h(0, 0, HALF, 3072)
+        quant_h(0, 0, HALF, 7 * BIG)
+        gate(3)
 
         def two(bank):
             return bank[:].rearrange("p (e c) -> p e c", e=2)
@@ -318,7 +319,7 @@ def tile_list_msg_silu_gateP_kernel(
         activate(1, 0, CHUNK, 2, rows[0])
         pack(1, 0, CHUNK, QIN_AT + 4 * QIN)
         quant_h(1, 0, CHUNK, WD_AT)
-        gate(0)
+        gate(0, 2)
         message(0, [0], banks[2])
         message(0, [1], banks[0])
         message(0, [2, 3], banks[5])
@@ -383,45 +384,54 @@ def tile_list_msg_silu_gateP_kernel(
 
         out_rows = out_0.rearrange("(p t) c -> p t c", t=PACK)
         quarters = T // QUARTER
-        pairs = [placed("pairs%d" % q, [P, 2, QUARTER, 2], BF16, 6 * BIG + q * QIN) for q in range(quarters)]
+        spans = [slice(0, CHUNK), slice(CHUNK, QUARTER)] + [slice(q * QUARTER, (q + 1) * QUARTER) for q in range(1, quarters)]
+        pairs = [
+            placed("pairs%d" % e, [P, 2, s.stop - s.start, 2], BF16, 6 * BIG + 8 * s.start) for e, s in enumerate(spans)
+        ]
 
-        def round_page(copy, t, q):
-            copy(pairs[q][:, t // 2, :, t % 2], pages[t][:, q * QUARTER : (q + 1) * QUARTER])
+        def round_page(copy, t, e):
+            copy(pairs[e][:, t // 2, :, t % 2], pages[t][:, spans[e]])
 
         for t in range(PACK):
             nc.sync.dma_start(out=out_rows[:, t, :], in_=pages[t][:])
-            for q in range(quarters):
-                round_page(nc.vector.tensor_copy if t >= 2 and q == 0 else nc.scalar.copy, t, q)
+            for e in range(len(spans)):
+                round_page(nc.vector.tensor_copy if t >= 2 and e < 2 else nc.scalar.copy, t, e)
         o_scales = keep.tile([P, 2 * QUARTER], U8, name="o_scales", align_bytes=64)
         out_words = out_1[0].rearrange("p c i -> p (c i)").bitcast(I32)
         o_bf = [placed("o_bf%d" % q, [P, PACK * QUARTER], BF16, TAB_AT + q * QIN) for q in range(quarters)]
         o_codes = [keep.tile([P, QUARTER], U32, name="o_codes%d" % q, align_bytes=64) for q in range(quarters)]
 
-        def weave(copy, q, c0, c1):
+        def weave(copy, e, c0, c1):
+            q, at = spans[e].start // QUARTER, spans[e].start % QUARTER
             dst = o_bf[q][:].bitcast(F32).rearrange("p (c k u) -> p c u k", k=2, u=2)
-            src = pairs[q][:].rearrange("p u c e -> p (u c e)").bitcast(F32).rearrange("p (u c k) -> p c u k", u=2, k=2)
-            copy(dst[:, c0 // 2 : c1 // 2], src[:, c0 // 2 : c1 // 2])
+            src = pairs[e][:].rearrange("p u c e -> p (u c e)").bitcast(F32).rearrange("p (u c k) -> p c u k", u=2, k=2)
+            copy(dst[:, (at + c0) // 2 : (at + c1) // 2], src[:, c0 // 2 : c1 // 2])
 
-        def quant_out(q, c0, c1):
+        def quant_out(q, c0, c1, s0=None):
             at = q % 2 * QUARTER
             nc.vector.quantize_mx(
                 out=o_codes[q][:, c0:c1].bitcast(FP8X4),
                 scales=o_scales[4 * (q // 2) : P, at + c0 : at + c1],
                 in_=o_bf[q][:, PACK * c0 : PACK * c1],
             )
-            nc.sync.dma_start(out=out_words[:, q * QUARTER + c0 : q * QUARTER + c1], in_=o_codes[q][:, c0:c1].bitcast(I32))
+            if s0 is not None:
+                nc.sync.dma_start(
+                    out=out_words[:, q * QUARTER + s0 : q * QUARTER + c1], in_=o_codes[q][:, s0:c1].bitcast(I32)
+                )
 
-        weave(nc.vector.tensor_copy, 0, 0, QUARTER)
-        weave(nc.vector.tensor_copy, 1, 0, QUARTER)
-        quant_out(0, 0, QUARTER)
-        weave(nc.vector.tensor_copy, 2, 0, CHUNK)
-        weave(nc.scalar.copy, 2, CHUNK, QUARTER)
-        quant_out(1, 0, QUARTER)
-        weave(nc.scalar.copy, 3, 0, CHUNK)
+        weave(nc.vector.tensor_copy, 0, 0, CHUNK)
+        weave(nc.vector.tensor_copy, 1, 0, CHUNK)
+        quant_out(0, 0, CHUNK)
+        weave(nc.vector.tensor_copy, 2, 0, QUARTER)
+        quant_out(0, CHUNK, QUARTER, 0)
+        weave(nc.vector.tensor_copy, 3, 0, CHUNK)
         weave(nc.scalar.copy, 3, CHUNK, QUARTER)
-        quant_out(2, 0, QUARTER)
-        quant_out(3, 0, CHUNK)
-        quant_out(3, CHUNK, QUARTER)
+        quant_out(1, 0, QUARTER, 0)
+        weave(nc.scalar.copy, 4, 0, CHUNK)
+        weave(nc.scalar.copy, 4, CHUNK, QUARTER)
+        quant_out(2, 0, QUARTER, 0)
+        quant_out(3, 0, CHUNK, 0)
+        quant_out(3, CHUNK, QUARTER, CHUNK)
         for q in range(4):
             (nc.scalar, nc.sync)[q % 2].dma_start(
                 out=out_2[0, 4 * q : 4 * q + 4, :].bitcast(I32).rearrange("r (g c) -> g r c", g=2),

@@ -21,22 +21,26 @@ P = 128
 PACK = 4
 PASS = P * PACK
 BANK = 512
-CHUNK = 256
-QUARTER = 512
-SCALAR_CASTS = 5
 HALF = J // 2
-BIG = 8192
-QIN = 4096
-QIN_SLOTS = 5
-TAB_AT = 8 * BIG
-QIN_AT = TAB_AT + 2 * BIG
-ROWS_AT = QIN_AT + QIN_SLOTS * QIN
-ACTS = 2
-A_BANKS = 3
-ACT_AT = ROWS_AT + 2 * QIN
-WD_AT = ACT_AT + ACTS * 2048
-SC_AT = WD_AT + QIN + 1024
-CH_AT = SC_AT + 3072
+CHUNK = J // 4
+QUARTER = T // 4
+SCALAR_CASTS = 5
+EARLY_SLOTS = 3
+FIRST_LOAD_PARTS = 4
+
+KB = 1024
+RAW = 8 * KB
+ROUNDED = 4 * KB
+TAB_AT = 8 * RAW
+ROUNDED_AT = TAB_AT + 2 * RAW
+ROUNDED_TILES = SCALAR_CASTS
+WIDE_ROWS_AT = ROUNDED_AT + ROUNDED_TILES * ROUNDED
+ACT_AT = WIDE_ROWS_AT + 2 * ROUNDED
+ACT_TILES = 2
+ACT = 2 * KB
+WD_AT = ACT_AT + ACT_TILES * ACT
+TAB_SCALES_AT = WD_AT + 5 * KB
+CHUNK_ROWS_AT = TAB_SCALES_AT + 3 * KB
 
 
 def tile_list_msg_silu_gateP_kernel(
@@ -51,19 +55,22 @@ def tile_list_msg_silu_gateP_kernel(
         def placed(name, shape, dtype, offset):
             return arena.tile(shape, dtype, name=name, align_bytes=64, offset=offset)
 
+        def kept(name, shape, dtype):
+            return keep.tile(shape, dtype, name=name, align_bytes=64)
+
         src_list = keep.tile([P, J // 16], U16, name="src_list")
         dst_list = keep.tile([P, J // 16], U16, name="dst_list")
         lists = (src_list, dst_list)
-        tab_sc = placed("tab_sc", [P, T], U8, SC_AT)
-        wd_sc_raw = keep.tile([P, N], U8, name="wd_sc_raw", align_bytes=64)
+        tab_sc = placed("tab_sc", [P, T], U8, TAB_SCALES_AT)
+        wd_sc_raw = kept("wd_sc_raw", [P, N], U8)
         nc.gpsimd.memset(tab_sc[:].bitcast(I32), 0)
         nc.gpsimd.memset(wd_sc_raw[:].bitcast(I32), 0)
         banks = [psum.tile([P, BANK], F32, name="bank%d" % i) for i in range(8)]
 
-        def load_scale_rows(queue, tile, scales):
-            for q in (0, 2, 1, 3):
-                queue.dma_start(
-                    out=tile[32 * q : 32 * q + 8, :].bitcast(I32), in_=scales[:, 4 * q : 4 * q + 4, :].bitcast(I32)
+        def load_scale_rows(tile, scales):
+            for g in (0, 2, 1, 3):
+                nc.sync.dma_start(
+                    out=tile[32 * g : 32 * g + 8, :].bitcast(I32), in_=scales[:, 4 * g : 4 * g + 4, :].bitcast(I32)
                 )
 
         warm = keep.tile([P, 2], F32, name="warm")
@@ -72,12 +79,12 @@ def tile_list_msg_silu_gateP_kernel(
         nc.sync.dma_start(src_list[:], offs)
         nc.sync.dma_start(dst_list[:], offs2)
 
-        tab_w = [placed("tab_w%d" % a, [P, T], I32, TAB_AT + a * BIG) for a in range(2)]
+        tab_w = [placed("tab_w%d" % a, [P, T], I32, TAB_AT + a * RAW) for a in range(2)]
 
         def load_tab(a, parts):
-            words = tab_words[a].rearrange("p t i -> p (t i)").bitcast(I32)
-            for q in range(parts):
-                cols = slice(q * T // parts, (q + 1) * T // parts)
+            words = tab_words[a].rearrange("p c i -> p (c i)").bitcast(I32)
+            for e in range(parts):
+                cols = slice(e * T // parts, (e + 1) * T // parts)
                 nc.sync.dma_start(out=tab_w[a][:, cols], in_=words[:, cols])
 
         pieces = [(b, side, a) for b in range(2) for a in range(2) for side in range(2)]
@@ -86,39 +93,40 @@ def tile_list_msg_silu_gateP_kernel(
         def load_piece(n):
             b, side, a = pieces[n]
             w = (ws, wt)[side]
-            raw[n] = placed("w_raw%d" % n, [P, PACK, PASS], F32, n * BIG)
+            raw[n] = placed("w_raw%d" % n, [P, PACK, PASS], F32, n * RAW)
             rows = w[a * PASS : (a + 1) * PASS, b * PASS : (b + 1) * PASS].rearrange("(p i) c -> p i c", i=PACK)
             nc.sync.dma_start(out=raw[n][:], in_=rows)
 
-        load_tab(0, 4)
+        load_tab(0, FIRST_LOAD_PARTS)
         wgo_row = keep.tile([P, J // P], F32, name="wgo_row")
         nc.sync.dma_start(out=wgo_row[:], in_=wgo[0].rearrange("(p e) -> p e", p=P))
         sm_sb = [keep.tile([P, PACK], F32, name="sm_sb%d" % b) for b in range(2)]
         sm_rows = sm.rearrange("(b p t) -> b p t", p=P, t=PACK)
         identity = keep.tile([P, P], F32, name="identity")
         make_identity(nc, identity[:])
-        load_scale_rows(nc.sync, tab_sc, tab_scales)
-        load_piece(0)
-        load_piece(1)
-        load_piece(2)
+        load_scale_rows(tab_sc, tab_scales)
+        for n in range(3):
+            load_piece(n)
         load_tab(1, 1)
-        g_rows = {}
-
-        def load_gate_rows(t):
-            g_rows[t] = placed("g_rows%d" % t, [P, T], F32, (4, 2, 1, 0)[t] * BIG)
-            nc.sync.dma_start(out=g_rows[t][:], in_=gT.rearrange("(p t) c -> p t c", t=PACK)[:, t, :])
-
         load_piece(3)
         load_piece(4)
         nc.sync.dma_start(out=sm_sb[0][:], in_=sm_rows[0])
         for n in range(5, 8):
             load_piece(n)
+
+        gate_at = {3: 0 * RAW, 2: 1 * RAW, 1: 2 * RAW, 0: 4 * RAW}
+        g_rows = {}
+
+        def load_gate_rows(t):
+            g_rows[t] = placed("g_rows%d" % t, [P, T], F32, gate_at[t])
+            nc.sync.dma_start(out=g_rows[t][:], in_=gT.rearrange("(p t) c -> p t c", t=PACK)[:, t, :])
+
         for t in (3, 2, 1):
             load_gate_rows(t)
         nc.sync.dma_start(out=sm_sb[1][:], in_=sm_rows[1])
         wd_raw = placed("wd_raw", [P, 2, N], I32, WD_AT)
         nc.sync.dma_start(out=wd_raw[:], in_=wd_words.rearrange("a p n i -> p a (n i)").bitcast(I32))
-        load_scale_rows(nc.sync, wd_sc_raw, wd_scales)
+        load_scale_rows(wd_sc_raw, wd_scales)
         load_gate_rows(0)
 
         wgo_sb = keep.tile([P, J], F32, name="wgo_sb")
@@ -138,19 +146,14 @@ def tile_list_msg_silu_gateP_kernel(
         v_words = {}
         v_scales = {}
 
-        def gather_words(side, a):
-            words = keep.tile([P, J], U32, name="v_words%d%d" % (side, a), align_bytes=64)
-            nc.vector.tensor_copy(words[:], tab_w[a][:].bitcast(U32).indirect(lists[side][:]))
-            v_words[side, a, 0] = words[:, 0:HALF]
-            v_words[side, a, 1] = words[:, HALF:J]
-
-        def gather_half(side, a, half, words):
-            offsets = lists[side][:, half * HALF // 16 : (half + 1) * HALF // 16]
+        def gather_words(side, a, halves, words):
+            offsets = lists[side][:, halves[0] * HALF // 16 : (halves[-1] + 1) * HALF // 16]
             nc.vector.tensor_copy(words[:], tab_w[a][:].bitcast(U32).indirect(offsets))
-            v_words[side, a, half] = words[:]
+            for e, half in enumerate(halves):
+                v_words[side, a, half] = words[:, e * HALF : (e + 1) * HALF]
 
         def gather_scales(side):
-            v_scales[side] = keep.tile([P, J], U8, name="v_scales%d" % side, align_bytes=64)
+            v_scales[side] = kept("v_scales%d" % side, [P, J], U8)
             nc.vector.tensor_copy(v_scales[side][:], tab_sc[:].indirect(lists[side][:]))
 
         w_codes = {}
@@ -158,7 +161,7 @@ def tile_list_msg_silu_gateP_kernel(
         w_bf = {}
 
         def cast_piece(n):
-            w_bf[n] = placed("w_bf%d" % n, [P, PACK * PASS], BF16, QIN_AT + n % QIN_SLOTS * QIN)
+            w_bf[n] = placed("w_bf%d" % n, [P, PACK * PASS], BF16, ROUNDED_AT + n % ROUNDED_TILES * ROUNDED)
             dst = w_bf[n][:].rearrange("p (u e m i) -> p u m i e", u=2, e=2, i=PACK)
             src = raw[n][:].rearrange("p i (m u e) -> p u m i e", u=2, e=2)
             if n < SCALAR_CASTS:
@@ -167,46 +170,45 @@ def tile_list_msg_silu_gateP_kernel(
                 for u in range(2):
                     nc.vector.tensor_copy(dst[:, u], src[:, u])
 
-        def quant_piece(n, at=None):
-            if at is None:
-                w_codes[n] = keep.tile([P, PASS], U32, name="w_codes%d" % n, align_bytes=64)
-            else:
-                w_codes[n] = placed("w_codes%d" % n, [P, PASS], U32, at)
-            w_scales[n] = keep.tile([P, PASS], U8, name="w_scales%d" % n, align_bytes=64)
+        def quant_piece(n, codes):
+            w_codes[n] = codes
+            w_scales[n] = kept("w_scales%d" % n, [P, PASS], U8)
             parts = 1 if n < SCALAR_CASTS else 2
             for u in range(parts):
                 cols = slice(u * PASS // parts, (u + 1) * PASS // parts)
                 nc.vector.quantize_mx(
-                    out=w_codes[n][:, cols].bitcast(FP8X4),
+                    out=codes[:, cols].bitcast(FP8X4),
                     scales=w_scales[n][:, cols],
                     in_=w_bf[n][:, PACK * cols.start : PACK * cols.stop],
                 )
 
-        gather_words(0, 0)
-        gather_words(1, 0)
-        gather_scales(0)
-        gather_scales(1)
-        for n in range(3):
+        def prepare_piece(n):
             cast_piece(n)
-            quant_piece(n, None)
+            quant_piece(n, kept("w_codes%d" % n, [P, PASS], U32))
+
         for side in range(2):
-            gather_half(side, 1, 0, keep.tile([P, HALF], U32, name="v_words%d10" % side, align_bytes=64))
-        cast_piece(3)
-        quant_piece(3)
+            gather_words(side, 0, [0, 1], kept("v_words%d0" % side, [P, J], U32))
         for side in range(2):
-            gather_half(side, 1, 1, placed("v_words%d11" % side, [P, HALF], U32, 3 * BIG + side * 2048))
+            gather_scales(side)
+        for n in range(3):
+            prepare_piece(n)
+        for side in range(2):
+            gather_words(side, 1, [0], kept("v_words%d10" % side, [P, HALF], U32))
+        prepare_piece(3)
+        for side in range(2):
+            gather_words(side, 1, [1], placed("v_words%d11" % side, [P, HALF], U32, 3 * RAW + side * 2 * KB))
 
         gates = {}
 
-        def gate(t, parts=1):
-            gates[t] = keep.tile([P, J], F32, name="gate%d" % t, align_bytes=64)
+        def gate(t, parts):
+            gates[t] = kept("gate%d" % t, [P, J], F32)
             for e in range(parts):
                 cols = slice(e * J // parts, (e + 1) * J // parts)
                 offsets = src_list[:, cols.start // 16 : cols.stop // 16]
                 nc.vector.tensor_tensor(gates[t][:, cols], g_rows[t][:].indirect(offsets), wgo_sb[:, cols], MULT)
 
-        wd_w = keep.tile([P, 2, N], I32, name="wd_w", align_bytes=64)
-        wd_sc = keep.tile([P, N], U8, name="wd_sc", align_bytes=64)
+        wd_w = kept("wd_w", [P, 2, N], I32)
+        wd_sc = kept("wd_sc", [P, N], U8)
 
         def sort_wd():
             nc.vector.tensor_copy(
@@ -220,18 +222,17 @@ def tile_list_msg_silu_gateP_kernel(
         h_codes = {}
         h_scales = {}
         h_rows = {}
-        turn = []
+        units = []
 
-        def activate(b, j0, width, t0, rows_at, act_at=None):
-            cols = slice(j0, j0 + width)
+        def next_act():
+            return ACT_AT + len(units) % ACT_TILES * ACT
+
+        def activate(b, j0, width, t0, bank, rows_at, act_at):
             per_bank = BANK // width
             if t0 == 0:
                 h_rows[b, j0] = placed("h_rows%d_%d" % (b, j0), [P, PACK, width], BF16, rows_at)
-            if act_at is None:
-                act_at = ACT_AT + len(turn) % ACTS * 2048
-            bank = banks[(0, 1, 2, 0, 1, 2, 0, 3, 1, 6, 7, 3, 1, 2, 3, 0)[len(turn)]]
-            act = placed("act%d" % len(turn), [P, BANK], F32, act_at)
-            turn.append(0)
+            act = placed("act%d" % len(units), [P, BANK], F32, act_at)
+            units.append((b, j0, t0))
             for s in range(4):
                 n = 4 * b + s
                 side, a = pieces[n][1:]
@@ -242,7 +243,7 @@ def tile_list_msg_silu_gateP_kernel(
                         lhsT=w_codes[n][:, rows].bitcast(FP8X4),
                         lhsT_scale=w_scales[n][:, rows],
                         rhs=v_words[side, a, j0 // HALF][:, j0 % HALF : j0 % HALF + width].bitcast(FP8X4),
-                        rhs_scale=v_scales[side][4 * a : P, cols],
+                        rhs_scale=v_scales[side][4 * a : P, j0 : j0 + width],
                         start=(s == 0 and u == 0),
                         stop=(s == 3 and u == per_bank - 1),
                     )
@@ -252,6 +253,10 @@ def tile_list_msg_silu_gateP_kernel(
                 nc.scalar.activation(
                     h_rows[b, j0][:, t, :], act[:, u * width : (u + 1) * width], COPY, scale=sm_sb[b][:, t : t + 1]
                 )
+
+        def activate_chunk(c, bank_pair, rows_at):
+            for e in range(2):
+                activate(1, c * CHUNK, CHUNK, 2 * e, bank_pair[e], rows_at, next_act())
 
         h_bf = {}
 
@@ -264,7 +269,7 @@ def tile_list_msg_silu_gateP_kernel(
 
         def quant_h(b, j0, width, at):
             h_codes[b, j0] = placed("h_codes%d_%d" % (b, j0), [P, width], U32, at)
-            h_scales[b, j0] = keep.tile([P, width], U8, name="h_scales%d_%d" % (b, j0), align_bytes=64)
+            h_scales[b, j0] = kept("h_scales%d_%d" % (b, j0), [P, width], U8)
             nc.vector.quantize_mx(out=h_codes[b, j0][:].bitcast(FP8X4), scales=h_scales[b, j0][:], in_=h_bf[b, j0][:])
 
         def message(c, slots, bank):
@@ -291,149 +296,133 @@ def tile_list_msg_silu_gateP_kernel(
                 MULT,
             )
 
-        low, high = slice(0, CHUNK), slice(CHUNK, BANK)
-        rows_a, rows_b, rows_c, rows_d = ROWS_AT, ROWS_AT + QIN, ROWS_AT + 2 * QIN, ROWS_AT + 2 * QIN + QIN // 2
-        cast_piece(4)
-        cast_piece(5)
-        quant_piece(5)
-        quant_piece(4, 5 * BIG)
-        for n in range(6, 8):
-            cast_piece(n)
-            quant_piece(n)
-        for t in range(PACK):
-            activate(0, 0, HALF, t, rows_a)
-        pack(0, 0, HALF, QIN_AT + 3 * QIN)
-        quant_h(0, 0, HALF, 7 * BIG)
-        gate(3)
+        def deliver(c, slots, bank, at):
+            y = placed("y%d_%d" % (c, slots[0]), [P, len(slots) * CHUNK], F32, at)
+            nc.scalar.copy(y[:], bank[:, 0 : len(slots) * CHUNK])
+            for e, t in enumerate(slots):
+                scatter(t, y[:, e * CHUNK : (e + 1) * CHUNK], c * CHUNK, CHUNK)
 
-        def two(bank):
+        def by_slot(bank):
             return bank[:].rearrange("p (e c) -> p e c", e=2)
 
-        rows = [CH_AT, CH_AT + 2048, CH_AT + QIN, CH_AT + QIN + 7168]
-        gate(2)
-        gate(1)
+        cast_piece(4)
+        prepare_piece(5)
+        quant_piece(4, placed("w_codes4", [P, PASS], U32, 5 * RAW))
+        for n in range(6, 8):
+            prepare_piece(n)
+
+        wide_rows = [WIDE_ROWS_AT + half * ROUNDED for half in range(2)]
+        chunk_rows = [CHUNK_ROWS_AT + at * KB for at in (0, 2, 4, 11)]
+        rounded = [ROUNDED_AT + e * ROUNDED for e in range(ROUNDED_TILES)]
+        last_gate = gate_at[0]
+
+        for t in range(PACK):
+            activate(0, 0, HALF, t, banks[len(units) % 3], wide_rows[0], next_act())
+        pack(0, 0, HALF, rounded[3])
+        for t in (3, 2, 1):
+            gate(t, 1)
         sort_wd()
-        for t in range(3):
-            activate(0, HALF, HALF, t, rows_b)
-        activate(1, 0, CHUNK, 0, rows[0])
-        activate(1, 0, CHUNK, 2, rows[0])
-        pack(1, 0, CHUNK, QIN_AT + 4 * QIN)
+        quant_h(0, 0, HALF, WD_AT + KB)
+        for t in range(EARLY_SLOTS):
+            activate(0, HALF, HALF, t, banks[len(units) % 3], wide_rows[1], next_act())
+        activate_chunk(0, (banks[3], banks[1]), chunk_rows[0])
+        pack(1, 0, CHUNK, rounded[4])
         quant_h(1, 0, CHUNK, WD_AT)
         gate(0, 2)
         message(0, [0], banks[2])
         message(0, [1], banks[0])
         message(0, [2, 3], banks[5])
-        activate(1, CHUNK, CHUNK, 0, rows[1])
-        activate(1, CHUNK, CHUNK, 2, rows[1])
-        pack(1, CHUNK, CHUNK, QIN_AT + 4 * QIN + QIN // 2)
-        y_00 = placed("y_00", [P, CHUNK], F32, rows[1])
-        nc.scalar.copy(y_00[:], banks[2][:, low])
-        scatter(0, y_00[:], 0, CHUNK)
-        quant_h(1, CHUNK, CHUNK, 4 * BIG)
-        y_10 = placed("y_10", [P, CHUNK], F32, 4 * BIG + 1024)
-        nc.scalar.copy(y_10[:], banks[0][:, low])
-        scatter(1, y_10[:], 0, CHUNK)
-        y_high0 = placed("y_high0", [P, BANK], F32, 4 * BIG + 2048)
-        nc.scalar.copy(y_high0[:], banks[5][:])
-        scatter(2, y_high0[:, low], 0, CHUNK)
-        scatter(3, y_high0[:, high], 0, CHUNK)
+        activate_chunk(1, (banks[6], banks[7]), chunk_rows[1])
+        pack(1, CHUNK, CHUNK, rounded[4] + ROUNDED // 2)
+        deliver(0, [0], banks[2], chunk_rows[1])
+        quant_h(1, CHUNK, CHUNK, last_gate)
+        deliver(0, [1], banks[0], last_gate + KB)
+        deliver(0, [2, 3], banks[5], last_gate + 2 * KB)
         message(1, [0, 1], banks[6])
         message(1, [2, 3], banks[7])
-        activate(0, HALF, HALF, 3, rows_b, 4 * BIG + QIN)
-        pack(0, HALF, HALF, QIN_AT)
-        quant_h(0, HALF, HALF, 5120)
-        y_low1 = placed("y_low1", [P, BANK], F32, rows_b)
-        nc.scalar.copy(y_low1[:], banks[6][:])
-        scatter(0, y_low1[:, low], CHUNK, CHUNK)
-        scatter(1, y_low1[:, high], CHUNK, CHUNK)
-
-        activate(1, 2 * CHUNK, CHUNK, 0, rows[2])
-        activate(1, 2 * CHUNK, CHUNK, 2, rows[2])
-        pack(1, 2 * CHUNK, CHUNK, QIN_AT + QIN)
-        quant_h(1, 2 * CHUNK, CHUNK, 7168)
-        y_late = placed("y_late", [P, 2, 3 * CHUNK], F32, rows[2] + 1024)
-        nc.scalar.copy(y_late[:, :, 0:CHUNK], two(banks[7]))
-        scatter(2, y_late[:, 0, 0:CHUNK], CHUNK, CHUNK)
-
+        activate(0, HALF, HALF, EARLY_SLOTS, banks[3], wide_rows[1], last_gate + 4 * KB)
+        pack(0, HALF, HALF, rounded[0])
+        quant_h(0, HALF, HALF, gate_at[3] + 5 * KB)
+        activate_chunk(2, (banks[1], banks[2]), chunk_rows[2])
+        deliver(1, [0, 1], banks[6], wide_rows[1])
+        pack(1, 2 * CHUNK, CHUNK, rounded[1])
+        quant_h(1, 2 * CHUNK, CHUNK, gate_at[3] + 7 * KB)
         message(2, [0], banks[2])
         message(2, [1], banks[4])
-        activate(1, 3 * CHUNK, CHUNK, 0, rows[3])
-        activate(1, 3 * CHUNK, CHUNK, 2, rows[3])
-        y_02 = placed("y_02", [P, CHUNK], F32, ACT_AT + (len(turn) - 1) % ACTS * 2048)
-        nc.scalar.copy(y_02[:], banks[2][:, low])
-        scatter(0, y_02[:], 2 * CHUNK, CHUNK)
-        pack(1, 3 * CHUNK, CHUNK, QIN_AT + QIN + QIN // 2)
-        quant_h(1, 3 * CHUNK, CHUNK, BIG)
-        y_12 = placed("y_12", [P, CHUNK], F32, rows[3])
-        nc.scalar.copy(y_12[:], banks[4][:, low])
-        scatter(1, y_12[:], 2 * CHUNK, CHUNK)
+        activate_chunk(3, (banks[3], banks[0]), chunk_rows[3])
+        y_late = placed("y_late", [P, 2, 3 * CHUNK], F32, chunk_rows[2] + KB)
+        nc.scalar.copy(y_late[:, :, 0:CHUNK], by_slot(banks[7]))
+        scatter(2, y_late[:, 0, 0:CHUNK], CHUNK, CHUNK)
+        deliver(2, [0], banks[2], next_act())
+        pack(1, 3 * CHUNK, CHUNK, rounded[1] + ROUNDED // 2)
+        quant_h(1, 3 * CHUNK, CHUNK, gate_at[2])
+        deliver(2, [1], banks[4], chunk_rows[3])
         message(3, [0], banks[5])
         message(3, [1], banks[6])
-        y_03 = placed("y_03", [P, CHUNK], F32, rows_a)
-        nc.scalar.copy(y_03[:], banks[5][:, low])
-        scatter(0, y_03[:], 3 * CHUNK, CHUNK)
-        y_13 = placed("y_13", [P, CHUNK], F32, rows_a + 1024)
-        nc.scalar.copy(y_13[:], banks[6][:, low])
-        scatter(1, y_13[:], 3 * CHUNK, CHUNK)
+        deliver(3, [0], banks[5], wide_rows[0])
+        deliver(3, [1], banks[6], wide_rows[0] + KB)
         message(2, [2, 3], banks[4])
         message(3, [2, 3], banks[2])
-        nc.scalar.copy(y_late[:, :, CHUNK : 2 * CHUNK], two(banks[4]))
-        nc.scalar.copy(y_late[:, :, 2 * CHUNK : 3 * CHUNK], two(banks[2]))
+        nc.scalar.copy(y_late[:, :, CHUNK : 2 * CHUNK], by_slot(banks[4]))
+        nc.scalar.copy(y_late[:, :, 2 * CHUNK : 3 * CHUNK], by_slot(banks[2]))
         scatter(2, y_late[:, 0, CHUNK : 3 * CHUNK], HALF, HALF)
-        scatter(PACK - 1, y_late[:, 1, :], CHUNK, 3 * CHUNK)
+        scatter(3, y_late[:, 1, :], CHUNK, 3 * CHUNK)
 
         out_rows = out_0.rearrange("(p t) c -> p t c", t=PACK)
         quarters = T // QUARTER
-        spans = [slice(0, CHUNK), slice(CHUNK, QUARTER)] + [slice(q * QUARTER, (q + 1) * QUARTER) for q in range(1, quarters)]
+        spans = [slice(0, QUARTER // 2), slice(QUARTER // 2, QUARTER)]
+        vector_spans = len(spans)
+        spans = spans + [slice(q * QUARTER, (q + 1) * QUARTER) for q in range(1, quarters)]
         pairs = [
-            placed("pairs%d" % e, [P, 2, s.stop - s.start, 2], BF16, 6 * BIG + 8 * s.start) for e, s in enumerate(spans)
+            placed("pairs%d" % e, [P, 2, s.stop - s.start, 2], BF16, 6 * RAW + 8 * s.start) for e, s in enumerate(spans)
         ]
-
-        def round_page(copy, t, e):
-            copy(pairs[e][:, t // 2, :, t % 2], pages[t][:, spans[e]])
-
         for t in range(PACK):
             nc.sync.dma_start(out=out_rows[:, t, :], in_=pages[t][:])
-            for e in range(len(spans)):
-                round_page(nc.vector.tensor_copy if t >= 2 and e < 2 else nc.scalar.copy, t, e)
-        o_scales = keep.tile([P, 2 * QUARTER], U8, name="o_scales", align_bytes=64)
+            for e, s in enumerate(spans):
+                copy = nc.vector.tensor_copy if t >= 2 and e < vector_spans else nc.scalar.copy
+                copy(pairs[e][:, t // 2, :, t % 2], pages[t][:, s])
+        o_scales = kept("o_scales", [P, T // 2], U8)
         out_words = out_1[0].rearrange("p c i -> p (c i)").bitcast(I32)
-        o_bf = [placed("o_bf%d" % q, [P, PACK * QUARTER], BF16, TAB_AT + q * QIN) for q in range(quarters)]
-        o_codes = [keep.tile([P, QUARTER], U32, name="o_codes%d" % q, align_bytes=64) for q in range(quarters)]
+        o_bf = [placed("o_bf%d" % q, [P, PACK * QUARTER], BF16, TAB_AT + q * ROUNDED) for q in range(quarters)]
+        o_codes = [kept("o_codes%d" % q, [P, QUARTER], U32) for q in range(quarters)]
 
-        def weave(copy, e, c0, c1):
-            q, at = spans[e].start // QUARTER, spans[e].start % QUARTER
+        def weave(copy, c0, c1):
+            e = [s.start <= c0 < s.stop for s in spans].index(True)
+            q, at, first = c0 // QUARTER, c0 % QUARTER, c0 - spans[e].start
             dst = o_bf[q][:].bitcast(F32).rearrange("p (c k u) -> p c u k", k=2, u=2)
             src = pairs[e][:].rearrange("p u c e -> p (u c e)").bitcast(F32).rearrange("p (u c k) -> p c u k", u=2, k=2)
-            copy(dst[:, (at + c0) // 2 : (at + c1) // 2], src[:, c0 // 2 : c1 // 2])
+            copy(dst[:, at // 2 : (at + c1 - c0) // 2], src[:, first // 2 : (first + c1 - c0) // 2])
 
-        def quant_out(q, c0, c1, s0=None):
-            at = q % 2 * QUARTER
+        def quant_out(c0, c1):
+            q, at = c0 // QUARTER, c0 % QUARTER
             nc.vector.quantize_mx(
-                out=o_codes[q][:, c0:c1].bitcast(FP8X4),
-                scales=o_scales[4 * (q // 2) : P, at + c0 : at + c1],
-                in_=o_bf[q][:, PACK * c0 : PACK * c1],
+                out=o_codes[q][:, at : at + c1 - c0].bitcast(FP8X4),
+                scales=o_scales[4 * (q // 2) : P, c0 % (T // 2) : c0 % (T // 2) + c1 - c0],
+                in_=o_bf[q][:, PACK * at : PACK * (at + c1 - c0)],
             )
-            if s0 is not None:
-                nc.sync.dma_start(
-                    out=out_words[:, q * QUARTER + s0 : q * QUARTER + c1], in_=o_codes[q][:, s0:c1].bitcast(I32)
-                )
 
-        weave(nc.vector.tensor_copy, 0, 0, CHUNK)
-        weave(nc.vector.tensor_copy, 1, 0, CHUNK)
-        quant_out(0, 0, CHUNK)
-        weave(nc.vector.tensor_copy, 2, 0, QUARTER)
-        quant_out(0, CHUNK, QUARTER, 0)
-        weave(nc.vector.tensor_copy, 3, 0, CHUNK)
-        weave(nc.scalar.copy, 3, CHUNK, QUARTER)
-        quant_out(1, 0, QUARTER, 0)
-        weave(nc.scalar.copy, 4, 0, CHUNK)
-        weave(nc.scalar.copy, 4, CHUNK, QUARTER)
-        quant_out(2, 0, QUARTER, 0)
-        quant_out(3, 0, CHUNK, 0)
-        quant_out(3, CHUNK, QUARTER, CHUNK)
-        for q in range(4):
-            (nc.scalar, nc.sync)[q % 2].dma_start(
-                out=out_2[0, 4 * q : 4 * q + 4, :].bitcast(I32).rearrange("r (g c) -> g r c", g=2),
-                in_=o_scales[32 * q : 32 * q + 8, :].bitcast(I32),
+        def store_codes(c0, c1):
+            q, at = c0 // QUARTER, c0 % QUARTER
+            nc.sync.dma_start(out=out_words[:, c0:c1], in_=o_codes[q][:, at : at + c1 - c0].bitcast(I32))
+
+        edge = [e * T // 8 for e in range(9)]
+        weave(nc.vector.tensor_copy, edge[0], edge[1])
+        weave(nc.vector.tensor_copy, edge[1], edge[2])
+        quant_out(edge[0], edge[1])
+        weave(nc.vector.tensor_copy, edge[2], edge[4])
+        quant_out(edge[1], edge[2])
+        store_codes(edge[0], edge[2])
+        weave(nc.vector.tensor_copy, edge[4], edge[5])
+        weave(nc.scalar.copy, edge[5], edge[6])
+        quant_out(edge[2], edge[4])
+        store_codes(edge[2], edge[4])
+        weave(nc.scalar.copy, edge[6], edge[7])
+        weave(nc.scalar.copy, edge[7], edge[8])
+        for c0, c1 in ((edge[4], edge[6]), (edge[6], edge[7]), (edge[7], edge[8])):
+            quant_out(c0, c1)
+            store_codes(c0, c1)
+        for g in range(4):
+            (nc.scalar, nc.sync)[g % 2].dma_start(
+                out=out_2[0, 4 * g : 4 * g + 4, :].bitcast(I32).rearrange("r (h c) -> h r c", h=2),
+                in_=o_scales[32 * g : 32 * g + 8, :].bitcast(I32),
             )

from contextlib import ExitStack

import concourse.mybir as mybir
from concourse.masks import make_identity

K, R, N, T, J = 1024, 1024, 512, 2048, 1024
FLOPS = 2 * (2 * K * R * J + R * N * J)

F32 = mybir.dt.float32
BF16 = mybir.dt.bfloat16
I32 = mybir.dt.int32
U32 = mybir.dt.uint32
U16 = mybir.dt.uint16
U8 = mybir.dt.uint8
FP8X4 = mybir.dt.float8_e4m3fn_x4
MULT = mybir.AluOpType.mult
SILU = mybir.ActivationFunctionType.Silu
COPY = mybir.ActivationFunctionType.Copy

P = 128
PACK = 4
PASS = P * PACK
BANK = 512
HALF = J // 2
CHUNK = J // 4
QUARTER = T // 4
SCALAR_CASTS = 5
EARLY_SLOTS = 3
FIRST_LOAD_PARTS = 4

KB = 1024
RAW = 8 * KB
ROUNDED = 4 * KB
TAB_AT = 8 * RAW
ROUNDED_AT = TAB_AT + 2 * RAW
ROUNDED_TILES = SCALAR_CASTS
WIDE_ROWS_AT = ROUNDED_AT + ROUNDED_TILES * ROUNDED
ACT_AT = WIDE_ROWS_AT + 2 * ROUNDED
ACT_TILES = 2
ACT = 2 * KB
WD_AT = ACT_AT + ACT_TILES * ACT
TAB_SCALES_AT = WD_AT + 5 * KB
CHUNK_ROWS_AT = TAB_SCALES_AT + 3 * KB


def tile_list_msg_silu_gateP_kernel(
    tc, tab_words, tab_scales, ws, wt, sm, wd_words, wd_scales, gT, wgo, offs, offs2, out_0, out_1, out_2
):
    nc = tc.nc
    with ExitStack() as ctx:
        keep = ctx.enter_context(tc.tile_pool(name="keep", bufs=1))
        arena = ctx.enter_context(tc.tile_pool(name="arena", bufs=1))
        psum = ctx.enter_context(tc.psum_pool(name="psum", bufs=1))

        def placed(name, shape, dtype, offset):
            return arena.tile(shape, dtype, name=name, align_bytes=64, offset=offset)

        def kept(name, shape, dtype):
            return keep.tile(shape, dtype, name=name, align_bytes=64)

        src_list = keep.tile([P, J // 16], U16, name="src_list")
        dst_list = keep.tile([P, J // 16], U16, name="dst_list")
        lists = (src_list, dst_list)
        tab_sc = placed("tab_sc", [P, T], U8, TAB_SCALES_AT)
        wd_sc_raw = kept("wd_sc_raw", [P, N], U8)
        nc.gpsimd.memset(tab_sc[:].bitcast(I32), 0)
        nc.gpsimd.memset(wd_sc_raw[:].bitcast(I32), 0)
        banks = [psum.tile([P, BANK], F32, name="bank%d" % i) for i in range(8)]

        def load_scale_rows(tile, scales):
            for g in (0, 2, 1, 3):
                nc.sync.dma_start(
                    out=tile[32 * g : 32 * g + 8, :].bitcast(I32), in_=scales[:, 4 * g : 4 * g + 4, :].bitcast(I32)
                )

        warm = keep.tile([P, 2], F32, name="warm")
        nc.vector.memset(warm[:], 0.0)
        nc.scalar.activation(warm[:, 1:2], warm[:, 0:1], SILU)
        nc.sync.dma_start(src_list[:], offs)
        nc.sync.dma_start(dst_list[:], offs2)

        tab_w = [placed("tab_w%d" % a, [P, T], I32, TAB_AT + a * RAW) for a in range(2)]

        def load_tab(a, parts):
            words = tab_words[a].rearrange("p c i -> p (c i)").bitcast(I32)
            for e in range(parts):
                cols = slice(e * T // parts, (e + 1) * T // parts)
                nc.sync.dma_start(out=tab_w[a][:, cols], in_=words[:, cols])

        pieces = [(b, side, a) for b in range(2) for a in range(2) for side in range(2)]
        raw = {}

        def load_piece(n):
            b, side, a = pieces[n]
            w = (ws, wt)[side]
            raw[n] = placed("w_raw%d" % n, [P, PACK, PASS], F32, n * RAW)
            rows = w[a * PASS : (a + 1) * PASS, b * PASS : (b + 1) * PASS].rearrange("(p i) c -> p i c", i=PACK)
            nc.sync.dma_start(out=raw[n][:], in_=rows)

        load_tab(0, FIRST_LOAD_PARTS)
        wgo_row = keep.tile([P, J // P], F32, name="wgo_row")
        nc.sync.dma_start(out=wgo_row[:], in_=wgo[0].rearrange("(p e) -> p e", p=P))
        sm_sb = [keep.tile([P, PACK], F32, name="sm_sb%d" % b) for b in range(2)]
        sm_rows = sm.rearrange("(b p t) -> b p t", p=P, t=PACK)
        identity = keep.tile([P, P], F32, name="identity")
        make_identity(nc, identity[:])
        load_scale_rows(tab_sc, tab_scales)
        for n in range(3):
            load_piece(n)
        load_tab(1, 1)
        load_piece(3)
        load_piece(4)
        nc.sync.dma_start(out=sm_sb[0][:], in_=sm_rows[0])
        for n in range(5, 8):
            load_piece(n)

        gate_at = {3: 0 * RAW, 2: 1 * RAW, 1: 2 * RAW, 0: 4 * RAW}
        g_rows = {}

        def load_gate_rows(t):
            g_rows[t] = placed("g_rows%d" % t, [P, T], F32, gate_at[t])
            nc.sync.dma_start(out=g_rows[t][:], in_=gT.rearrange("(p t) c -> p t c", t=PACK)[:, t, :])

        for t in (3, 2, 1):
            load_gate_rows(t)
        nc.sync.dma_start(out=sm_sb[1][:], in_=sm_rows[1])
        wd_raw = placed("wd_raw", [P, 2, N], I32, WD_AT)
        nc.sync.dma_start(out=wd_raw[:], in_=wd_words.rearrange("a p n i -> p a (n i)").bitcast(I32))
        load_scale_rows(wd_sc_raw, wd_scales)
        load_gate_rows(0)

        wgo_sb = keep.tile([P, J], F32, name="wgo_sb")
        for half in range(2):
            spread = banks[4 + half][:].rearrange("q (e p) -> q e p", e=PACK)
            for e in range(PACK):
                column = PACK * half + e
                nc.tensor.transpose(spread[:, e, :], wgo_row[:, column : column + 1].to_broadcast([P, P]), identity[:])
            nc.scalar.copy(
                wgo_sb[:].rearrange("q (p h e) -> q h p e", h=2, e=PACK)[:, half], spread.rearrange("q e p -> q p e")
            )

        pages = [keep.tile([P, T], F32, name="page%d" % t) for t in range(PACK)]
        for t in range(PACK):
            nc.vector.memset(pages[t][:].bitcast(I32), 0)

        v_words = {}
        v_scales = {}

        def gather_words(side, a, halves, words):
            offsets = lists[side][:, halves[0] * HALF // 16 : (halves[-1] + 1) * HALF // 16]
            nc.vector.tensor_copy(words[:], tab_w[a][:].bitcast(U32).indirect(offsets))
            for e, half in enumerate(halves):
                v_words[side, a, half] = words[:, e * HALF : (e + 1) * HALF]

        def gather_scales(side):
            v_scales[side] = kept("v_scales%d" % side, [P, J], U8)
            nc.vector.tensor_copy(v_scales[side][:], tab_sc[:].indirect(lists[side][:]))

        w_codes = {}
        w_scales = {}
        w_bf = {}

        def cast_piece(n):
            w_bf[n] = placed("w_bf%d" % n, [P, PACK * PASS], BF16, ROUNDED_AT + n % ROUNDED_TILES * ROUNDED)
            dst = w_bf[n][:].rearrange("p (u e m i) -> p u m i e", u=2, e=2, i=PACK)
            src = raw[n][:].rearrange("p i (m u e) -> p u m i e", u=2, e=2)
            if n < SCALAR_CASTS:
                nc.scalar.copy(dst, src)
            else:
                for u in range(2):
                    nc.vector.tensor_copy(dst[:, u], src[:, u])

        def quant_piece(n, codes):
            w_codes[n] = codes
            w_scales[n] = kept("w_scales%d" % n, [P, PASS], U8)
            parts = 1 if n < SCALAR_CASTS else 2
            for u in range(parts):
                cols = slice(u * PASS // parts, (u + 1) * PASS // parts)
                nc.vector.quantize_mx(
                    out=codes[:, cols].bitcast(FP8X4),
                    scales=w_scales[n][:, cols],
                    in_=w_bf[n][:, PACK * cols.start : PACK * cols.stop],
                )

        def prepare_piece(n):
            cast_piece(n)
            quant_piece(n, kept("w_codes%d" % n, [P, PASS], U32))

        for side in range(2):
            gather_words(side, 0, [0, 1], kept("v_words%d0" % side, [P, J], U32))
        for side in range(2):
            gather_scales(side)
        for n in range(3):
            prepare_piece(n)
        for side in range(2):
            gather_words(side, 1, [0], kept("v_words%d10" % side, [P, HALF], U32))
        prepare_piece(3)
        for side in range(2):
            gather_words(side, 1, [1], placed("v_words%d11" % side, [P, HALF], U32, 3 * RAW + side * 2 * KB))

        gates = {}

        def gate(t, parts):
            gates[t] = kept("gate%d" % t, [P, J], F32)
            for e in range(parts):
                cols = slice(e * J // parts, (e + 1) * J // parts)
                offsets = src_list[:, cols.start // 16 : cols.stop // 16]
                nc.vector.tensor_tensor(gates[t][:, cols], g_rows[t][:].indirect(offsets), wgo_sb[:, cols], MULT)

        wd_w = kept("wd_w", [P, 2, N], I32)
        wd_sc = kept("wd_sc", [P, N], U8)

        def sort_wd():
            nc.vector.tensor_copy(
                wd_w[:].rearrange("p a (u e m) -> p u a m e", u=2, e=2),
                wd_raw[:].rearrange("p a (m u e) -> p u a m e", u=2, e=2),
            )
            nc.vector.tensor_copy(
                wd_sc[:].rearrange("p (t m) -> p t m", t=PACK), wd_sc_raw[:].rearrange("p (m t) -> p t m", t=PACK)
            )

        h_codes = {}
        h_scales = {}
        h_rows = {}
        units = []

        def next_act():
            return ACT_AT + len(units) % ACT_TILES * ACT

        def activate(b, j0, width, t0, bank, rows_at, act_at):
            per_bank = BANK // width
            if t0 == 0:
                h_rows[b, j0] = placed("h_rows%d_%d" % (b, j0), [P, PACK, width], BF16, rows_at)
            act = placed("act%d" % len(units), [P, BANK], F32, act_at)
            units.append((b, j0, t0))
            for s in range(4):
                n = 4 * b + s
                side, a = pieces[n][1:]
                for u in range(per_bank):
                    rows = slice((t0 + u) * P, (t0 + u + 1) * P)
                    nc.tensor.matmul_mx(
                        out=bank[:, u * width : (u + 1) * width],
                        lhsT=w_codes[n][:, rows].bitcast(FP8X4),
                        lhsT_scale=w_scales[n][:, rows],
                        rhs=v_words[side, a, j0 // HALF][:, j0 % HALF : j0 % HALF + width].bitcast(FP8X4),
                        rhs_scale=v_scales[side][4 * a : P, j0 : j0 + width],
                        start=(s == 0 and u == 0),
                        stop=(s == 3 and u == per_bank - 1),
                    )
            nc.scalar.activation(act[:], bank[:], SILU)
            for u in range(per_bank):
                t = t0 + u
                nc.scalar.activation(
                    h_rows[b, j0][:, t, :], act[:, u * width : (u + 1) * width], COPY, scale=sm_sb[b][:, t : t + 1]
                )

        def activate_chunk(c, bank_pair, rows_at):
            for e in range(2):
                activate(1, c * CHUNK, CHUNK, 2 * e, bank_pair[e], rows_at, next_act())

        h_bf = {}

        def pack(b, j0, width, at):
            h_bf[b, j0] = placed("h_bf%d_%d" % (b, j0), [P, PACK * width], BF16, at)
            nc.scalar.copy(
                h_bf[b, j0][:].rearrange("p (c i t) -> p c t i", i=4, t=PACK),
                h_rows[b, j0][:].rearrange("p t (c i) -> p c t i", i=4),
            )

        def quant_h(b, j0, width, at):
            h_codes[b, j0] = placed("h_codes%d_%d" % (b, j0), [P, width], U32, at)
            h_scales[b, j0] = kept("h_scales%d_%d" % (b, j0), [P, width], U8)
            nc.vector.quantize_mx(out=h_codes[b, j0][:].bitcast(FP8X4), scales=h_scales[b, j0][:], in_=h_bf[b, j0][:])

        def message(c, slots, bank):
            for e, t in enumerate(slots):
                rows = slice(t * P, (t + 1) * P)
                for b in range(2):
                    j0 = c * CHUNK if b else c * CHUNK // HALF * HALF
                    cols = slice(c * CHUNK - j0, (c + 1) * CHUNK - j0)
                    nc.tensor.matmul_mx(
                        out=bank[:, e * CHUNK : (e + 1) * CHUNK],
                        lhsT=wd_w[:, b, rows].bitcast(FP8X4),
                        lhsT_scale=wd_sc[4 * b : P, rows],
                        rhs=h_codes[b, j0][:, cols].bitcast(FP8X4),
                        rhs_scale=h_scales[b, j0][:, cols],
                        start=(b == 0),
                        stop=(b == 1),
                    )

        def scatter(t, y, j0, width):
            nc.vector.tensor_tensor(
                pages[t][:].indirect(dst_list[:, j0 // 16 : (j0 + width) // 16]),
                y,
                gates[t][:, j0 : j0 + width],
                MULT,
            )

        def deliver(c, slots, bank, at):
            y = placed("y%d_%d" % (c, slots[0]), [P, len(slots) * CHUNK], F32, at)
            nc.scalar.copy(y[:], bank[:, 0 : len(slots) * CHUNK])
            for e, t in enumerate(slots):
                scatter(t, y[:, e * CHUNK : (e + 1) * CHUNK], c * CHUNK, CHUNK)

        def by_slot(bank):
            return bank[:].rearrange("p (e c) -> p e c", e=2)

        cast_piece(4)
        prepare_piece(5)
        quant_piece(4, placed("w_codes4", [P, PASS], U32, 5 * RAW))
        for n in range(6, 8):
            prepare_piece(n)

        wide_rows = [WIDE_ROWS_AT + half * ROUNDED for half in range(2)]
        chunk_rows = [CHUNK_ROWS_AT + at * KB for at in (0, 2, 4, 11)]
        rounded = [ROUNDED_AT + e * ROUNDED for e in range(ROUNDED_TILES)]
        last_gate = gate_at[0]

        for t in range(PACK):
            activate(0, 0, HALF, t, banks[len(units) % 3], wide_rows[0], next_act())
        pack(0, 0, HALF, rounded[3])
        for t in (3, 2, 1):
            gate(t, 1)
        sort_wd()
        quant_h(0, 0, HALF, WD_AT + KB)
        for t in range(EARLY_SLOTS):
            activate(0, HALF, HALF, t, banks[len(units) % 3], wide_rows[1], next_act())
        activate_chunk(0, (banks[3], banks[1]), chunk_rows[0])
        pack(1, 0, CHUNK, rounded[4])
        quant_h(1, 0, CHUNK, WD_AT)
        gate(0, 2)
        message(0, [0], banks[2])
        message(0, [1], banks[0])
        message(0, [2, 3], banks[5])
        activate_chunk(1, (banks[6], banks[7]), chunk_rows[1])
        pack(1, CHUNK, CHUNK, rounded[4] + ROUNDED // 2)
        deliver(0, [0], banks[2], chunk_rows[1])
        quant_h(1, CHUNK, CHUNK, last_gate)
        deliver(0, [1], banks[0], last_gate + KB)
        deliver(0, [2, 3], banks[5], last_gate + 2 * KB)
        message(1, [0, 1], banks[6])
        message(1, [2, 3], banks[7])
        activate(0, HALF, HALF, EARLY_SLOTS, banks[3], wide_rows[1], last_gate + 4 * KB)
        pack(0, HALF, HALF, rounded[0])
        quant_h(0, HALF, HALF, gate_at[3] + 5 * KB)
        activate_chunk(2, (banks[1], banks[2]), chunk_rows[2])
        deliver(1, [0, 1], banks[6], wide_rows[1])
        pack(1, 2 * CHUNK, CHUNK, rounded[1])
        quant_h(1, 2 * CHUNK, CHUNK, gate_at[3] + 7 * KB)
        message(2, [0], banks[2])
        message(2, [1], banks[4])
        activate_chunk(3, (banks[3], banks[0]), chunk_rows[3])
        y_late = placed("y_late", [P, 2, 3 * CHUNK], F32, chunk_rows[2] + KB)
        nc.scalar.copy(y_late[:, :, 0:CHUNK], by_slot(banks[7]))
        scatter(2, y_late[:, 0, 0:CHUNK], CHUNK, CHUNK)
        deliver(2, [0], banks[2], next_act())
        pack(1, 3 * CHUNK, CHUNK, rounded[1] + ROUNDED // 2)
        quant_h(1, 3 * CHUNK, CHUNK, gate_at[2])
        deliver(2, [1], banks[4], chunk_rows[3])
        message(3, [0], banks[5])
        message(3, [1], banks[6])
        deliver(3, [0], banks[5], wide_rows[0])
        deliver(3, [1], banks[6], wide_rows[0] + KB)
        message(2, [2, 3], banks[4])
        message(3, [2, 3], banks[2])
        nc.scalar.copy(y_late[:, :, CHUNK : 2 * CHUNK], by_slot(banks[4]))
        nc.scalar.copy(y_late[:, :, 2 * CHUNK : 3 * CHUNK], by_slot(banks[2]))
        scatter(2, y_late[:, 0, CHUNK : 3 * CHUNK], HALF, HALF)
        scatter(3, y_late[:, 1, :], CHUNK, 3 * CHUNK)

        out_rows = out_0.rearrange("(p t) c -> p t c", t=PACK)
        quarters = T // QUARTER
        spans = [slice(0, QUARTER // 2), slice(QUARTER // 2, QUARTER)]
        vector_spans = len(spans)
        spans = spans + [slice(q * QUARTER, (q + 1) * QUARTER) for q in range(1, quarters)]
        pairs = [
            placed("pairs%d" % e, [P, 2, s.stop - s.start, 2], BF16, 6 * RAW + 8 * s.start) for e, s in enumerate(spans)
        ]
        for t in range(PACK):
            nc.sync.dma_start(out=out_rows[:, t, :], in_=pages[t][:])
            for e, s in enumerate(spans):
                copy = nc.vector.tensor_copy if t >= 2 and e < vector_spans else nc.scalar.copy
                copy(pairs[e][:, t // 2, :, t % 2], pages[t][:, s])
        o_scales = kept("o_scales", [P, T // 2], U8)
        out_words = out_1[0].rearrange("p c i -> p (c i)").bitcast(I32)
        o_bf = [placed("o_bf%d" % q, [P, PACK * QUARTER], BF16, TAB_AT + q * ROUNDED) for q in range(quarters)]
        o_codes = [kept("o_codes%d" % q, [P, QUARTER], U32) for q in range(quarters)]

        def weave(copy, c0, c1):
            e = [s.start <= c0 < s.stop for s in spans].index(True)
            q, at, first = c0 // QUARTER, c0 % QUARTER, c0 - spans[e].start
            dst = o_bf[q][:].bitcast(F32).rearrange("p (c k u) -> p c u k", k=2, u=2)
            src = pairs[e][:].rearrange("p u c e -> p (u c e)").bitcast(F32).rearrange("p (u c k) -> p c u k", u=2, k=2)
            copy(dst[:, at // 2 : (at + c1 - c0) // 2], src[:, first // 2 : (first + c1 - c0) // 2])

        def quant_out(c0, c1):
            q, at = c0 // QUARTER, c0 % QUARTER
            nc.vector.quantize_mx(
                out=o_codes[q][:, at : at + c1 - c0].bitcast(FP8X4),
                scales=o_scales[4 * (q // 2) : P, c0 % (T // 2) : c0 % (T // 2) + c1 - c0],
                in_=o_bf[q][:, PACK * at : PACK * (at + c1 - c0)],
            )

        def store_codes(c0, c1):
            q, at = c0 // QUARTER, c0 % QUARTER
            nc.sync.dma_start(out=out_words[:, c0:c1], in_=o_codes[q][:, at : at + c1 - c0].bitcast(I32))

        edge = [e * T // 8 for e in range(9)]
        weave(nc.vector.tensor_copy, edge[0], edge[1])
        weave(nc.vector.tensor_copy, edge[1], edge[2])
        quant_out(edge[0], edge[1])
        weave(nc.vector.tensor_copy, edge[2], edge[4])
        quant_out(edge[1], edge[2])
        store_codes(edge[0], edge[2])
        weave(nc.vector.tensor_copy, edge[4], edge[5])
        weave(nc.scalar.copy, edge[5], edge[6])
        quant_out(edge[2], edge[4])
        store_codes(edge[2], edge[4])
        weave(nc.scalar.copy, edge[6], edge[7])
        weave(nc.scalar.copy, edge[7], edge[8])
        for c0, c1 in ((edge[4], edge[6]), (edge[6], edge[7]), (edge[7], edge[8])):
            quant_out(c0, c1)
            store_codes(c0, c1)
        for g in range(4):
            (nc.scalar, nc.sync)[g % 2].dma_start(
                out=out_2[0, 4 * g : 4 * g + 4, :].bitcast(I32).rearrange("r (h c) -> h r c", h=2),
                in_=o_scales[32 * g : 32 * g + 8, :].bitcast(I32),
            )
